import numpy as np
import ml_dtypes


def mxq(x, axis, fmt="e4m3"):
    dtype, down = {"e4m3": (ml_dtypes.float8_e4m3fn, 7), "e5m2": (ml_dtypes.float8_e5m2, 14)}[fmt]
    v = np.moveaxis(np.asarray(x, np.float32).astype(ml_dtypes.bfloat16).astype(np.float64), axis, -1)
    blocks = v.reshape(v.shape[:-1] + (-1, 32))
    amax = np.abs(blocks).max(-1, keepdims=True)
    byte = np.maximum(np.where(amax > 0, np.frexp(amax)[1] - 1 + 127, 0) - down, 1)
    scale = np.exp2(byte - 127.0)
    codes = (blocks / scale).astype(np.float32).astype(dtype).astype(np.float64)
    return np.moveaxis((codes * scale).reshape(v.shape), -1, axis)


WIDE = False


def mx_kscale(k):
    if not WIDE:
        return np.ones(k)
    levels = np.array([30, -30])
    if k % 512:
        return np.exp2(np.random.permutation(np.resize(levels, k // 32))).repeat(32)
    a = np.empty((k // 512, 16))
    for p in range(k // 512):
        a[p, :8] = np.random.permutation(np.resize(levels, 8))
        for g in range(8):
            far = levels[np.abs(levels - a[p, g]) >= 10]
            a[p, g + 8] = far[np.random.randint(len(far))]
    return np.exp2(a.ravel()).repeat(32)


def f64(x):
    return np.asarray(x).astype(np.float64)


E2M1 = np.array([0.0, 0.5, 1.0, 1.5, 2.0, 3.0, 4.0, 6.0, -0.0, -0.5, -1.0, -1.5, -2.0, -3.0, -4.0, -6.0])


def pack_weight(w, fmt):
    k, n = w.shape
    w = f64(np.asarray(w, np.float32).astype(ml_dtypes.bfloat16)).reshape(k // 32, 32, n)
    amax = np.abs(w).max(1)
    if fmt == "e4m3":
        byte = np.frexp(amax)[1] - 1 + 127 - 7
    else:
        mant, ex = np.frexp(amax / 6.0)
        byte = np.where(mant > 0.5, ex, ex - 1) + 127
    byte = np.clip(np.where(amax > 0, byte, 1), 1, 254)
    scaled = (w * np.exp2(127.0 - byte)[:, None, :]).reshape(k, n).astype(np.float32)
    by_word = np.ascontiguousarray(scaled.reshape(k // 512, 128, 4, n).transpose(0, 1, 3, 2))
    if fmt == "e4m3":
        words = by_word.astype(ml_dtypes.float8_e4m3fn).view(np.uint8)
    else:
        c = by_word.astype(ml_dtypes.float4_e2m1fn).view(np.uint8) & 0xF
        words = (c[..., 0::2] | (c[..., 1::2] << 4)).reshape(k // 512, 128, 2 * n)
    return np.ascontiguousarray(words), np.ascontiguousarray(byte.astype(np.uint8).reshape(k // 512, 16, n))


def unpack_weight(words, scales, fmt):
    g, _, n = scales.shape
    words = np.ascontiguousarray(words).reshape(g, 128, n, -1)
    if fmt == "e4m3":
        vals = words.view(ml_dtypes.float8_e4m3fn).astype(np.float64)
    else:
        nib = np.empty((g, 128, n, 4), np.uint8)
        nib[..., 0::2] = words & 0xF
        nib[..., 1::2] = words >> 4
        vals = E2M1[nib]
    vals = vals * np.repeat(np.exp2(scales.astype(np.float64) - 127.0), 8, axis=1)[..., None]
    return vals.transpose(0, 1, 3, 2).reshape(g * 512, n)


def planes(y):
    n, m = y.shape
    v = y.astype(np.float32).astype(ml_dtypes.bfloat16).astype(np.float64).reshape(n // 32, 32, m)
    top = np.abs(v).max(1)
    byte = np.clip(np.where(top > 0, np.frexp(top)[1] - 1 + 127 - 7, 1), 1, 254)
    codes = (v * np.exp2(127.0 - byte)[:, None, :]).reshape(n, m).astype(np.float32).astype(ml_dtypes.float8_e4m3fn).view(np.uint8)
    words = codes.reshape(n // 512, 128, 4, m).transpose(0, 1, 3, 2)
    return np.ascontiguousarray(words), np.ascontiguousarray(byte.astype(np.uint8).reshape(n // 512, 16, m))


K, L, R, M, T = 1024, 1536, 1024, 512, 512


def setup_inputs():
    n = np.random.standard_normal
    s1 = mx_kscale(K)[:, None]
    s2 = mx_kscale(L)[:, None]
    u = mx_kscale(R)[:, None]
    p_w = pack_weight(n((R, M)) / np.sqrt(R) / u, "e2m1")
    return {
        "x": (n((K, T)) * s1).astype(np.float32),
        "wx": (n((K, R)) / np.sqrt(K) / s1 * u.T).astype(np.float32),
        "c": (n((L, T)) * s2).astype(np.float32),
        "wc": (n((L, R)) / np.sqrt(L) / s2).astype(np.float32),
        "w_words": p_w[0],
        "w_scales": p_w[1],
        "prev": (n((512, 512))).astype(np.float32),
    }


def reference(x, wx, c, wc, w_words, w_scales, prev):
    x_ = mxq(f64(x), 0, "e4m3")
    wx_ = mxq(f64(wx), 0, "e4m3")
    c_ = mxq(f64(c), 0, "e5m2")
    wc_ = mxq(f64(wc), 0, "e4m3")
    w_ = unpack_weight(w_words, w_scales, "e2m1")
    h_ = mxq((wx_.T @ x_) * (wc_.T @ c_), 0, "e4m3")
    y = h_.T @ w_
    out_0 = f64(prev) + y
    return (out_0,) + planes(out_0)

@@ -1,0 +1,281 @@
+from contextlib import ExitStack
+
+import concourse.mybir as mybir
+
+K, L, R, M, T = 1024, 1536, 1024, 512, 512
+FLOPS = 2 * T * (K * R + L * R + R * M)
+
+F32 = mybir.dt.float32
+BF16 = mybir.dt.bfloat16
+U32 = mybir.dt.uint32
+I32 = mybir.dt.int32
+U8 = mybir.dt.uint8
+E4M3 = mybir.dt.float8_e4m3fn_x4
+E5M2 = mybir.dt.float8_e5m2_x4
+E2M1 = mybir.dt.float4_e2m1fn_x4
+ALU = mybir.AluOpType
+
+P = 128
+PACK = 4
+PASS = P * PACK
+WIDE = 512
+
+
+def tile_mix_bilin_tm_pl_res_kernel(tc, x, wx, c, wc, w_words, w_scales, prev, out_0, out_1, out_2):
+    nc = tc.nc
+    with ExitStack() as ctx:
+        sb = ctx.enter_context(tc.tile_pool(name="sb", bufs=1))
+        ps = ctx.enter_context(tc.psum_pool(name="ps", bufs=1))
+        ctx.enter_context(tc.manual_schedule())
+
+        banks = [ps.tile([P, WIDE], F32, name="bank%d" % b) for b in range(8)]
+        banks_a, banks_b = banks[:4], banks[4:]
+
+        def rows(src, g, c0, c1):
+            return src[g * PASS:(g + 1) * PASS, c0:c1].rearrange("(p j) w -> p j w", j=PACK)
+
+        keys = []
+        for g in range(3):
+            keys += [("c", g, 0), ("wc", g, 0), ("wc", g, 1)]
+        keys += [("x", 0, 0), ("wx", 0, 0), ("x", 1, 0), ("wx", 1, 0), ("wx", 0, 1), ("wx", 1, 1)]
+
+        w_code = sb.tile([P, 2, 2 * M], U8, name="w_code", align_bytes=64)
+        w_scale = sb.tile([P, 2, M], U8, name="w_scale", align_bytes=64)
+        nc.gpsimd.memset(w_scale[:].rearrange("p a n -> p (a n)").bitcast(I32), 0)
+        for q in range(4):
+            nc.scalar.dma_start(
+                out=w_scale[32 * q:32 * q + 4].bitcast(I32),
+                in_=w_scales[:, 4 * q:4 * q + 4, :].rearrange("a r n -> r a n").bitcast(I32),
+            )
+
+        raw, codes, scales = {}, {}, {}
+        res = sb.tile([P, PACK, M], F32, name="res", align_bytes=64)
+        for n, key in enumerate(keys):
+            codes[key] = sb.tile([P, WIDE], U32, name="codes%d" % n, align_bytes=64)
+            scales[key] = sb.tile([P, WIDE], U8, name="scales%d" % n, align_bytes=64)
+
+        def load(name, src, g, c0, c1):
+            tile = sb.tile([P, PACK, c1 - c0], F32, name="raw_%s%d_%d" % (name, g, c0), align_bytes=64)
+            nc.sync.dma_start(out=tile[:], in_=rows(src, g, c0, c1))
+            return tile
+
+
+        for g in range(3):
+            raw[("c", g, 0)] = load("c", c, g, 0, T)[:]
+            both = load("wc", wc, g, 0, R)
+            raw[("wc", g, 0)] = both[:, :, :WIDE]
+            raw[("wc", g, 1)] = both[:, :, WIDE:]
+        for g in range(2):
+            raw[("x", g, 0)] = load("x", x, g, 0, T)[:]
+            raw[("wx", g, 0)] = load("wx", wx, g, 0, WIDE)[:]
+        raw[("wx", 0, 1)] = load("wx", wx, 0, WIDE, R)[:]
+        nc.sync.dma_start(out=w_code[:].bitcast(I32), in_=w_words.rearrange("a p n -> p a n").bitcast(I32))
+        raw[("wx", 1, 1)] = load("wx", wx, 1, WIDE, R)[:]
+        nc.sync.dma_start(out=res[:], in_=prev.rearrange("(p i) n -> p i n", i=PACK))
+
+        staged = [sb.tile([P, PACK, P, PACK], BF16, name="staged%d" % n, align_bytes=64) for n in range(4)]
+        stage_of = {key: staged[n % 4] for n, key in enumerate(keys)}
+
+        def cast_part(copy, src, dst, s0, s1):
+            copy(
+                out=dst[:, s0:s1].rearrange("p s m j -> p m j s"),
+                in_=src.rearrange("p j (m s) -> p m j s", s=PACK)[:, :, :, s0:s1],
+            )
+
+        def cast_v(key, s0=0, s1=2):
+            cast_part(nc.vector.tensor_copy, raw[key], stage_of[key][:], s0, s1)
+
+        def cast_s(key, s0=2, s1=4):
+            cast_part(nc.scalar.copy, raw[key], stage_of[key][:], s0, s1)
+
+        def quant_half(key, u, s):
+            cols = slice(s * P + 64 * u, s * P + 64 * (u + 1))
+            nc.vector.quantize_mx(
+                out=codes[key][:, cols].bitcast(E4M3),
+                scales=scales[key][:, cols],
+                in_=stage_of[key][:, s, 64 * u:64 * (u + 1)].rearrange("p m j -> p (m j)"),
+            )
+
+        def quant(key, s0=0, s1=4):
+            fmt = E5M2 if key[0] == "c" else E4M3
+            nc.vector.quantize_mx(
+                out=codes[key][:, s0 * P:s1 * P].bitcast(fmt),
+                scales=scales[key][:, s0 * P:s1 * P],
+                in_=stage_of[key][:, s0:s1].rearrange("p s m j -> p (s m j)"),
+            )
+
+        def pc_pass(a, g):
+            for j in range(PACK):
+                cols = slice(j * P, (j + 1) * P)
+                nc.tensor.matmul_mx(
+                    out=banks[4 * a + j][:],
+                    lhsT=codes[("wc", g, a)][:, cols].bitcast(E4M3),
+                    lhsT_scale=scales[("wc", g, a)][:, cols],
+                    rhs=codes[("c", g, 0)][:].bitcast(E5M2),
+                    rhs_scale=scales[("c", g, 0)][:],
+                    start=(g == 0),
+                    stop=(g == 2),
+                )
+
+        pc_sb = [sb.tile([P, PACK, T], F32, name="pc_sb%d" % a, align_bytes=64) for a in range(2)]
+
+        def pc_copy(a, j):
+            nc.scalar.copy(out=pc_sb[a][:, j], in_=banks[4 * a + j][:])
+
+        def px_bank(a, i, bank):
+            tcols = slice(i * P, (i + 1) * P)
+            for j in range(PACK):
+                cols = slice(j * P, (j + 1) * P)
+                for g in range(2):
+                    nc.tensor.matmul_mx(
+                        out=bank[:, cols],
+                        lhsT=codes[("wx", g, a)][:, cols].bitcast(E4M3),
+                        lhsT_scale=scales[("wx", g, a)][:, cols],
+                        rhs=codes[("x", g, 0)][:, tcols].bitcast(E4M3),
+                        rhs_scale=scales[("x", g, 0)][:, tcols],
+                        start=(g == 0),
+                        stop=(g == 1),
+                    )
+
+        h_bf = [sb.tile([P, PACK, P * PACK], BF16, name="h_bf%d" % a, align_bytes=64) for a in range(2)]
+        h_code = [sb.tile([P, T], U32, name="h_code%d" % a, align_bytes=64) for a in range(2)]
+        h_scale = [sb.tile([P, T], U8, name="h_scale%d" % a, align_bytes=64) for a in range(2)]
+
+        def h_mult(a, i, bank):
+            nc.vector.tensor_tensor(
+                out=h_bf[a][:, i].rearrange("p (u e j) -> p u j e", e=4, j=PACK),
+                in0=bank[:].rearrange("p (j u e) -> p u j e", j=PACK, e=4),
+                in1=pc_sb[a][:, :, i * P:(i + 1) * P].rearrange("p j (u e) -> p u j e", e=4),
+                op=ALU.mult,
+            )
+
+        def h_quant(a, i0, i1):
+            nc.vector.quantize_mx(
+                out=h_code[a][:, i0 * P:i1 * P].bitcast(E4M3),
+                scales=h_scale[a][:, i0 * P:i1 * P],
+                in_=h_bf[a][:, i0:i1].rearrange("p i w -> p (i w)"),
+            )
+
+        def y_pass(a, i):
+            cols = slice(i * P, (i + 1) * P)
+            nc.tensor.matmul_mx(
+                out=banks_b[i][:],
+                lhsT=h_code[a][:, cols].bitcast(E4M3),
+                lhsT_scale=h_scale[a][:, cols],
+                rhs=w_code[:, a].bitcast(E2M1),
+                rhs_scale=w_scale[:, a],
+                start=(a == 0),
+                stop=(a == 1),
+            )
+
+        out_rows = out_0.rearrange("(p i) n -> p i n", i=PACK)
+
+        def y_add(i, n0, n1):
+            nc.vector.tensor_tensor(out=res[:, i, n0:n1], in0=banks_b[i][:, n0:n1], in1=res[:, i, n0:n1], op=ALU.add)
+
+        def store_res(n0, n1):
+            nc.sync.dma_start(out=out_rows[:, :, n0:n1], in_=res[:, :, n0:n1])
+
+        def shared(key):
+            cast_v(key)
+            cast_s(key)
+
+        o_bf = sb.tile([P, M * PACK], BF16, name="o_bf", align_bytes=64)
+        o_code = sb.tile([P, M], U32, name="o_code", align_bytes=64)
+        o_scale = sb.tile([P, M], U8, name="o_scale", align_bytes=64)
+        words = out_1[0].rearrange("p n i -> p (n i)").bitcast(I32)
+
+        def o_cast(copy, n0, n1):
+            copy(
+                out=o_bf[:, n0 * PACK:n1 * PACK].rearrange("p (u e i) -> p u i e", e=4, i=PACK),
+                in_=res[:, :, n0:n1].rearrange("p i (u e) -> p u i e", e=4),
+            )
+
+        def o_quant(n0, n1):
+            nc.vector.quantize_mx(out=o_code[:, n0:n1].bitcast(E4M3), scales=o_scale[:, n0:n1], in_=o_bf[:, n0 * PACK:n1 * PACK])
+
+        def store_words(n0, n1):
+            nc.sync.dma_start(out=words[:, n0:n1], in_=o_code[:, n0:n1].bitcast(I32))
+
+
+        def urgent(key):
+            cut = 96
+            cast_v(key)
+            cast_part(nc.scalar.copy, raw[key][:, :, :cut * PACK], stage_of[key][:, :, :cut], 2, 4)
+            cast_part(nc.vector.tensor_copy, raw[key][:, :, cut * PACK:], stage_of[key][:, :, cut:], 2, 4)
+            quant(key, 0, 2)
+            quant(key, 2, 4)
+
+        for g in range(3):
+            shared(("c", g, 0))
+            quant(("c", g, 0))
+            shared(("wc", g, 0))
+            cast_v(("wc", g, 1))
+            quant(("wc", g, 0))
+            pc_pass(0, g)
+            cast_s(("wc", g, 1))
+            quant(("wc", g, 1))
+            pc_pass(1, g)
+        cast_v(("x", 0, 0), 0, 4)
+        for j in range(PACK):
+            pc_copy(0, j)
+        quant(("x", 0, 0))
+        cast_v(("wx", 0, 0), 0, 4)
+        pc_copy(1, 0)
+        pc_copy(1, 1)
+        quant(("wx", 0, 0))
+        shared(("x", 1, 0))
+        pc_copy(1, 2)
+        pc_copy(1, 3)
+        quant(("x", 1, 0))
+        urgent(("wx", 1, 0))
+        for i in range(PACK):
+            px_bank(0, i, banks_a[i])
+        cast_s(("wx", 0, 1), 0, 4)
+        h_mult(0, 0, banks_a[0])
+        h_mult(0, 1, banks_a[1])
+        h_mult(0, 2, banks_a[2])
+        h_mult(0, 3, banks_a[3])
+        h_quant(0, 0, 2)
+        y_pass(0, 0)
+        y_pass(0, 1)
+        quant(("wx", 0, 1))
+        urgent(("wx", 1, 1))
+
+        for i in range(PACK):
+            px_bank(1, i, banks_a[i])
+        h_quant(0, 2, 4)
+        h_mult(1, 0, banks_a[0])
+        h_mult(1, 1, banks_a[1])
+        h_quant(1, 0, 1)
+        y_pass(1, 0)
+        h_mult(1, 2, banks_a[2])
+        h_quant(1, 1, 2)
+        y_pass(1, 1)
+        h_mult(1, 3, banks_a[3])
+        h_quant(1, 2, 3)
+        y_pass(0, 2)
+        y_pass(1, 2)
+        y_add(0, 0, 512)
+        nc.sync.dma_start(out=out_rows[:, 0], in_=res[:, 0])
+        h_quant(1, 3, 4)
+        y_pass(0, 3)
+        y_pass(1, 3)
+        y_add(1, 0, 512)
+        nc.sync.dma_start(out=out_rows[:, 1], in_=res[:, 1])
+        y_add(2, 0, 256)
+        y_add(3, 0, 256)
+        o_cast(nc.scalar.copy, 0, 192)
+        y_add(2, 256, 512)
+        nc.sync.dma_start(out=out_rows[:, 2], in_=res[:, 2])
+        y_add(3, 256, 512)
+        nc.sync.dma_start(out=out_rows[:, 3], in_=res[:, 3])
+        o_cast(nc.vector.tensor_copy, 192, 256)
+        o_cast(nc.vector.tensor_copy, 256, 512)
+        o_quant(0, 256)
+        store_words(0, 256)
+        o_quant(256, 512)
+        store_words(256, 512)
+        for q in range(4):
+            eng = nc.sync if q % 2 == 0 else nc.scalar
+            eng.dma_start(out=out_2[0, 4 * q:4 * q + 4, :].bitcast(I32), in_=o_scale[32 * q:32 * q + 4, :].bitcast(I32))

@@ -36,17 +36,12 @@ def tile_mix_bilin_tm_pl_res_kernel(tc, x, wx, c, wc, w_words, w_scales, prev, o
 
         keys = []
         for g in range(3):
-            keys += [("c", g, 0), ("wc", g, 0), ("wc", g, 1)]
+            keys += [("wc", g, 0), ("wc", g, 1), ("c", g, 0)]
         keys += [("x", 0, 0), ("wx", 0, 0), ("x", 1, 0), ("wx", 1, 0), ("wx", 0, 1), ("wx", 1, 1)]
 
         w_code = sb.tile([P, 2, 2 * M], U8, name="w_code", align_bytes=64)
         w_scale = sb.tile([P, 2, M], U8, name="w_scale", align_bytes=64)
         nc.gpsimd.memset(w_scale[:].rearrange("p a n -> p (a n)").bitcast(I32), 0)
-        for q in range(4):
-            nc.scalar.dma_start(
-                out=w_scale[32 * q:32 * q + 4].bitcast(I32),
-                in_=w_scales[:, 4 * q:4 * q + 4, :].rearrange("a r n -> r a n").bitcast(I32),
-            )
 
         raw, codes, scales = {}, {}, {}
         res = sb.tile([P, PACK, M], F32, name="res", align_bytes=64)
@@ -61,16 +56,21 @@ def tile_mix_bilin_tm_pl_res_kernel(tc, x, wx, c, wc, w_words, w_scales, prev, o
 
 
         for g in range(3):
-            raw[("c", g, 0)] = load("c", c, g, 0, T)[:]
             both = load("wc", wc, g, 0, R)
             raw[("wc", g, 0)] = both[:, :, :WIDE]
             raw[("wc", g, 1)] = both[:, :, WIDE:]
+            raw[("c", g, 0)] = load("c", c, g, 0, T)[:]
         for g in range(2):
             raw[("x", g, 0)] = load("x", x, g, 0, T)[:]
             raw[("wx", g, 0)] = load("wx", wx, g, 0, WIDE)[:]
         raw[("wx", 0, 1)] = load("wx", wx, 0, WIDE, R)[:]
-        nc.sync.dma_start(out=w_code[:].bitcast(I32), in_=w_words.rearrange("a p n -> p a n").bitcast(I32))
         raw[("wx", 1, 1)] = load("wx", wx, 1, WIDE, R)[:]
+        nc.sync.dma_start(out=w_code[:].bitcast(I32), in_=w_words.rearrange("a p n -> p a n").bitcast(I32))
+        for q in range(4):
+            nc.sync.dma_start(
+                out=w_scale[32 * q:32 * q + 4].bitcast(I32),
+                in_=w_scales[:, 4 * q:4 * q + 4, :].rearrange("a r n -> r a n").bitcast(I32),
+            )
         nc.sync.dma_start(out=res[:], in_=prev.rearrange("(p i) n -> p i n", i=PACK))
 
         staged = [sb.tile([P, PACK, P, PACK], BF16, name="staged%d" % n, align_bytes=64) for n in range(4)]
@@ -198,59 +198,72 @@ def tile_mix_bilin_tm_pl_res_kernel(tc, x, wx, c, wc, w_words, w_scales, prev, o
             nc.sync.dma_start(out=words[:, n0:n1], in_=o_code[:, n0:n1].bitcast(I32))
 
 
-        def urgent(key):
-            cut = 96
+        def urgent(key, cut):
             cast_v(key)
             cast_part(nc.scalar.copy, raw[key][:, :, :cut * PACK], stage_of[key][:, :, :cut], 2, 4)
             cast_part(nc.vector.tensor_copy, raw[key][:, :, cut * PACK:], stage_of[key][:, :, cut:], 2, 4)
             quant(key, 0, 2)
             quant(key, 2, 4)
 
+        def warm(count, wkey, xkey, bank):
+            for n in range(count):
+                nc.tensor.matmul_mx(
+                    out=bank[:],
+                    lhsT=codes[wkey][:, :P].bitcast(E4M3),
+                    lhsT_scale=scales[wkey][:, :P],
+                    rhs=codes[xkey][:].bitcast(E4M3),
+                    rhs_scale=scales[xkey][:],
+                    start=True,
+                    stop=True,
+                )
+
         for g in range(3):
+            shared(("wc", g, 0))
+            shared(("wc", g, 1))
+            quant(("wc", g, 0))
+            quant(("wc", g, 1))
             shared(("c", g, 0))
             quant(("c", g, 0))
-            shared(("wc", g, 0))
-            cast_v(("wc", g, 1))
-            quant(("wc", g, 0))
             pc_pass(0, g)
-            cast_s(("wc", g, 1))
-            quant(("wc", g, 1))
             pc_pass(1, g)
         cast_v(("x", 0, 0), 0, 4)
         for j in range(PACK):
             pc_copy(0, j)
         quant(("x", 0, 0))
         cast_v(("wx", 0, 0), 0, 4)
-        pc_copy(1, 0)
-        pc_copy(1, 1)
+        for j in range(PACK):
+            pc_copy(1, j)
         quant(("wx", 0, 0))
-        shared(("x", 1, 0))
-        pc_copy(1, 2)
-        pc_copy(1, 3)
+        warm(3, ("wx", 0, 0), ("x", 0, 0), banks_a[3])
+        cast_v(("x", 1, 0), 0, 4)
         quant(("x", 1, 0))
-        urgent(("wx", 1, 0))
+        warm(3, ("wx", 0, 0), ("x", 1, 0), banks_a[3])
+        urgent(("wx", 1, 0), 96)
         for i in range(PACK):
             px_bank(0, i, banks_a[i])
         cast_s(("wx", 0, 1), 0, 4)
         h_mult(0, 0, banks_a[0])
         h_mult(0, 1, banks_a[1])
         h_mult(0, 2, banks_a[2])
+        warm(2, ("wx", 0, 0), ("x", 0, 0), banks_a[2])
         h_mult(0, 3, banks_a[3])
-        h_quant(0, 0, 2)
-        y_pass(0, 0)
-        y_pass(0, 1)
+        warm(2, ("wx", 0, 0), ("x", 0, 0), banks_a[3])
+        shared(("wx", 1, 1))
         quant(("wx", 0, 1))
-        urgent(("wx", 1, 1))
+        quant(("wx", 1, 1), 0, 2)
+        quant(("wx", 1, 1), 2, 4)
 
         for i in range(PACK):
             px_bank(1, i, banks_a[i])
-        h_quant(0, 2, 4)
+        h_quant(0, 0, 4)
         h_mult(1, 0, banks_a[0])
         h_mult(1, 1, banks_a[1])
         h_quant(1, 0, 1)
+        y_pass(0, 0)
         y_pass(1, 0)
         h_mult(1, 2, banks_a[2])
         h_quant(1, 1, 2)
+        y_pass(0, 1)
         y_pass(1, 1)
         h_mult(1, 3, banks_a[3])
         h_quant(1, 2, 3)

@@ -198,12 +198,15 @@ def tile_mix_bilin_tm_pl_res_kernel(tc, x, wx, c, wc, w_words, w_scales, prev, o
             nc.sync.dma_start(out=words[:, n0:n1], in_=o_code[:, n0:n1].bitcast(I32))
 
 
-        def urgent(key, cut):
+        def split(key, cut):
             cast_v(key)
             cast_part(nc.scalar.copy, raw[key][:, :, :cut * PACK], stage_of[key][:, :, :cut], 2, 4)
-            cast_part(nc.vector.tensor_copy, raw[key][:, :, cut * PACK:], stage_of[key][:, :, cut:], 2, 4)
-            quant(key, 0, 2)
-            quant(key, 2, 4)
+            if cut < P:
+                cast_part(nc.vector.tensor_copy, raw[key][:, :, cut * PACK:], stage_of[key][:, :, cut:], 2, 4)
+
+        def cast_g(out, in_):
+            nc.gpsimd.tensor_scalar(out=out, in0=in_, scalar1=1.0, scalar2=0.0, op0=ALU.mult, op1=ALU.add)
+
 
         def warm(count, wkey, xkey, bank):
             for n in range(count):
@@ -218,38 +221,50 @@ def tile_mix_bilin_tm_pl_res_kernel(tc, x, wx, c, wc, w_words, w_scales, prev, o
                 )
 
         for g in range(3):
-            shared(("wc", g, 0))
-            shared(("wc", g, 1))
+            split(("wc", g, 0), 96)
+            split(("wc", g, 1), 96)
             quant(("wc", g, 0))
             quant(("wc", g, 1))
-            shared(("c", g, 0))
+            split(("c", g, 0), 96)
             quant(("c", g, 0))
             pc_pass(0, g)
             pc_pass(1, g)
-        cast_v(("x", 0, 0), 0, 4)
+        split(("x", 0, 0), 96)
         for j in range(PACK):
             pc_copy(0, j)
         quant(("x", 0, 0))
         cast_v(("wx", 0, 0), 0, 4)
-        for j in range(PACK):
-            pc_copy(1, j)
+        pc_copy(1, 0)
+        pc_copy(1, 1)
         quant(("wx", 0, 0))
         warm(3, ("wx", 0, 0), ("x", 0, 0), banks_a[3])
-        cast_v(("x", 1, 0), 0, 4)
+        split(("x", 1, 0), 96)
+        pc_copy(1, 2)
         quant(("x", 1, 0))
         warm(3, ("wx", 0, 0), ("x", 1, 0), banks_a[3])
-        urgent(("wx", 1, 0), 96)
+        split(("wx", 1, 0), 92)
+        quant(("wx", 1, 0), 0, 2)
+        quant(("wx", 1, 0), 2, 4)
+        pc_copy(1, 3)
         for i in range(PACK):
             px_bank(0, i, banks_a[i])
-        cast_s(("wx", 0, 1), 0, 4)
+        cast_s(("wx", 0, 1), 1, 4)
+        reuse = stage_of[("wx", 1, 0)][:, 3]
+        cast_g(reuse, raw[("wx", 0, 1)].rearrange("p j (m s) -> p m j s", s=PACK)[:, :, :, 0])
         h_mult(0, 0, banks_a[0])
         h_mult(0, 1, banks_a[1])
         h_mult(0, 2, banks_a[2])
         warm(2, ("wx", 0, 0), ("x", 0, 0), banks_a[2])
         h_mult(0, 3, banks_a[3])
         warm(2, ("wx", 0, 0), ("x", 0, 0), banks_a[3])
-        shared(("wx", 1, 1))
-        quant(("wx", 0, 1))
+        split(("wx", 1, 1), 120)
+        nc.vector.quantize_mx(
+            out=codes[("wx", 0, 1)][:, :P].bitcast(E4M3),
+            scales=scales[("wx", 0, 1)][:, :P],
+            in_=reuse.rearrange("p m j -> p (m j)"),
+        )
+        quant(("wx", 0, 1), 1, 2)
+        quant(("wx", 0, 1), 2, 4)
         quant(("wx", 1, 1), 0, 2)
         quant(("wx", 1, 1), 2, 4)
 
@@ -278,12 +293,12 @@ def tile_mix_bilin_tm_pl_res_kernel(tc, x, wx, c, wc, w_words, w_scales, prev, o
         nc.sync.dma_start(out=out_rows[:, 1], in_=res[:, 1])
         y_add(2, 0, 256)
         y_add(3, 0, 256)
-        o_cast(nc.scalar.copy, 0, 192)
+        o_cast(nc.scalar.copy, 0, 176)
         y_add(2, 256, 512)
         nc.sync.dma_start(out=out_rows[:, 2], in_=res[:, 2])
         y_add(3, 256, 512)
         nc.sync.dma_start(out=out_rows[:, 3], in_=res[:, 3])
-        o_cast(nc.vector.tensor_copy, 192, 256)
+        o_cast(nc.vector.tensor_copy, 176, 256)
         o_cast(nc.vector.tensor_copy, 256, 512)
         o_quant(0, 256)
         store_words(0, 256)

@@ -122,20 +122,19 @@ def tile_mix_bilin_tm_pl_res_kernel(tc, x, wx, c, wc, w_words, w_scales, prev, o
         def pc_copy(a, j):
             nc.scalar.copy(out=pc_sb[a][:, j], in_=banks[4 * a + j][:])
 
-        def px_bank(a, i, bank):
+        def px_pass(a, g, i, j0=0, j1=PACK):
             tcols = slice(i * P, (i + 1) * P)
-            for j in range(PACK):
+            for j in range(j0, j1):
                 cols = slice(j * P, (j + 1) * P)
-                for g in range(2):
-                    nc.tensor.matmul_mx(
-                        out=bank[:, cols],
-                        lhsT=codes[("wx", g, a)][:, cols].bitcast(E4M3),
-                        lhsT_scale=scales[("wx", g, a)][:, cols],
-                        rhs=codes[("x", g, 0)][:, tcols].bitcast(E4M3),
-                        rhs_scale=scales[("x", g, 0)][:, tcols],
-                        start=(g == 0),
-                        stop=(g == 1),
-                    )
+                nc.tensor.matmul_mx(
+                    out=banks_a[i][:, cols],
+                    lhsT=codes[("wx", g, a)][:, cols].bitcast(E4M3),
+                    lhsT_scale=scales[("wx", g, a)][:, cols],
+                    rhs=codes[("x", g, 0)][:, tcols].bitcast(E4M3),
+                    rhs_scale=scales[("x", g, 0)][:, tcols],
+                    start=(g == 0 and j == 0),
+                    stop=(g == 1 and j == PACK - 1),
+                )
 
         h_bf = [sb.tile([P, PACK, P * PACK], BF16, name="h_bf%d" % a, align_bytes=64) for a in range(2)]
         h_code = [sb.tile([P, T], U32, name="h_code%d" % a, align_bytes=64) for a in range(2)]
@@ -237,27 +236,27 @@ def tile_mix_bilin_tm_pl_res_kernel(tc, x, wx, c, wc, w_words, w_scales, prev, o
         pc_copy(1, 0)
         pc_copy(1, 1)
         quant(("wx", 0, 0))
-        warm(3, ("wx", 0, 0), ("x", 0, 0), banks_a[3])
+        for i in range(PACK):
+            px_pass(0, 0, i)
         split(("x", 1, 0), 96)
         pc_copy(1, 2)
+        pc_copy(1, 3)
         quant(("x", 1, 0))
-        warm(3, ("wx", 0, 0), ("x", 1, 0), banks_a[3])
-        split(("wx", 1, 0), 92)
+        warm(3, ("wx", 0, 0), ("x", 1, 0), banks_b[0])
+        split(("wx", 1, 0), 96)
         quant(("wx", 1, 0), 0, 2)
         quant(("wx", 1, 0), 2, 4)
-        pc_copy(1, 3)
         for i in range(PACK):
-            px_bank(0, i, banks_a[i])
+            px_pass(0, 1, i)
         cast_s(("wx", 0, 1), 1, 4)
         reuse = stage_of[("wx", 1, 0)][:, 3]
         cast_g(reuse, raw[("wx", 0, 1)].rearrange("p j (m s) -> p m j s", s=PACK)[:, :, :, 0])
         h_mult(0, 0, banks_a[0])
         h_mult(0, 1, banks_a[1])
+        warm(2, ("wx", 0, 0), ("x", 0, 0), banks_a[1])
         h_mult(0, 2, banks_a[2])
         warm(2, ("wx", 0, 0), ("x", 0, 0), banks_a[2])
         h_mult(0, 3, banks_a[3])
-        warm(2, ("wx", 0, 0), ("x", 0, 0), banks_a[3])
-        split(("wx", 1, 1), 120)
         nc.vector.quantize_mx(
             out=codes[("wx", 0, 1)][:, :P].bitcast(E4M3),
             scales=scales[("wx", 0, 1)][:, :P],
@@ -265,11 +264,14 @@ def tile_mix_bilin_tm_pl_res_kernel(tc, x, wx, c, wc, w_words, w_scales, prev, o
         )
         quant(("wx", 0, 1), 1, 2)
         quant(("wx", 0, 1), 2, 4)
+        for i in range(PACK):
+            px_pass(1, 0, i)
+        split(("wx", 1, 1), 96)
         quant(("wx", 1, 1), 0, 2)
         quant(("wx", 1, 1), 2, 4)
 
         for i in range(PACK):
-            px_bank(1, i, banks_a[i])
+            px_pass(1, 1, i)
         h_quant(0, 0, 4)
         h_mult(1, 0, banks_a[0])
         h_mult(1, 1, banks_a[1])

@@ -37,7 +37,7 @@ def tile_mix_bilin_tm_pl_res_kernel(tc, x, wx, c, wc, w_words, w_scales, prev, o
         keys = []
         for g in range(3):
             keys += [("wc", g, 0), ("wc", g, 1), ("c", g, 0)]
-        keys += [("x", 0, 0), ("wx", 0, 0), ("x", 1, 0), ("wx", 1, 0), ("wx", 0, 1), ("wx", 1, 1)]
+        keys += [("x", 0, 0), ("wx", 0, 0), ("wx", 1, 0), ("x", 1, 0), ("wx", 0, 1), ("wx", 1, 1)]
 
         w_code = sb.tile([P, 2, 2 * M], U8, name="w_code", align_bytes=64)
         w_scale = sb.tile([P, 2, M], U8, name="w_scale", align_bytes=64)
@@ -60,9 +60,10 @@ def tile_mix_bilin_tm_pl_res_kernel(tc, x, wx, c, wc, w_words, w_scales, prev, o
             raw[("wc", g, 0)] = both[:, :, :WIDE]
             raw[("wc", g, 1)] = both[:, :, WIDE:]
             raw[("c", g, 0)] = load("c", c, g, 0, T)[:]
-        for g in range(2):
-            raw[("x", g, 0)] = load("x", x, g, 0, T)[:]
-            raw[("wx", g, 0)] = load("wx", wx, g, 0, WIDE)[:]
+        raw[("x", 0, 0)] = load("x", x, 0, 0, T)[:]
+        raw[("wx", 0, 0)] = load("wx", wx, 0, 0, WIDE)[:]
+        raw[("wx", 1, 0)] = load("wx", wx, 1, 0, WIDE)[:]
+        raw[("x", 1, 0)] = load("x", x, 1, 0, T)[:]
         raw[("wx", 0, 1)] = load("wx", wx, 0, WIDE, R)[:]
         raw[("wx", 1, 1)] = load("wx", wx, 1, WIDE, R)[:]
         nc.sync.dma_start(out=w_code[:].bitcast(I32), in_=w_words.rearrange("a p n -> p a n").bitcast(I32))
@@ -238,32 +239,35 @@ def tile_mix_bilin_tm_pl_res_kernel(tc, x, wx, c, wc, w_words, w_scales, prev, o
         quant(("wx", 0, 0))
         for i in range(PACK):
             px_pass(0, 0, i)
-        split(("x", 1, 0), 96)
+        split(("wx", 1, 0), 96)
         pc_copy(1, 2)
         pc_copy(1, 3)
-        quant(("x", 1, 0))
-        warm(3, ("wx", 0, 0), ("x", 1, 0), banks_b[0])
-        split(("wx", 1, 0), 96)
-        quant(("wx", 1, 0), 0, 2)
-        quant(("wx", 1, 0), 2, 4)
+        quant(("wx", 1, 0))
+        warm(3, ("wx", 1, 0), ("x", 0, 0), banks_b[0])
+        cast_v(("x", 1, 0), 0, 1)
+        cast_v(("x", 1, 0), 1, 2)
+        cast_s(("x", 1, 0), 2, 4)
+        quant(("x", 1, 0), 0, 1)
+        quant(("x", 1, 0), 1, 2)
+        quant(("x", 1, 0), 2, 4)
         for i in range(PACK):
             px_pass(0, 1, i)
-        cast_s(("wx", 0, 1), 1, 4)
-        reuse = stage_of[("wx", 1, 0)][:, 3]
-        cast_g(reuse, raw[("wx", 0, 1)].rearrange("p j (m s) -> p m j s", s=PACK)[:, :, :, 0])
+        cast_s(("wx", 0, 1), 2, 4)
+        g_stage = sb.tile([P, 2, P, PACK], BF16, name="g_stage", align_bytes=64)
+        for s in range(2):
+            cast_g(g_stage[:, s], raw[("wx", 0, 1)].rearrange("p j (m s) -> p m j s", s=PACK)[:, :, :, s])
         h_mult(0, 0, banks_a[0])
         h_mult(0, 1, banks_a[1])
         warm(2, ("wx", 0, 0), ("x", 0, 0), banks_a[1])
         h_mult(0, 2, banks_a[2])
         warm(2, ("wx", 0, 0), ("x", 0, 0), banks_a[2])
         h_mult(0, 3, banks_a[3])
-        nc.vector.quantize_mx(
-            out=codes[("wx", 0, 1)][:, :P].bitcast(E4M3),
-            scales=scales[("wx", 0, 1)][:, :P],
-            in_=reuse.rearrange("p m j -> p (m j)"),
-        )
-        quant(("wx", 0, 1), 1, 2)
         quant(("wx", 0, 1), 2, 4)
+        nc.vector.quantize_mx(
+            out=codes[("wx", 0, 1)][:, :2 * P].bitcast(E4M3),
+            scales=scales[("wx", 0, 1)][:, :2 * P],
+            in_=g_stage[:].rearrange("p s m j -> p (s m j)"),
+        )
         for i in range(PACK):
             px_pass(1, 0, i)
         split(("wx", 1, 1), 96)

@@ -244,37 +244,35 @@ def tile_mix_bilin_tm_pl_res_kernel(tc, x, wx, c, wc, w_words, w_scales, prev, o
         pc_copy(1, 3)
         quant(("wx", 1, 0))
         warm(3, ("wx", 1, 0), ("x", 0, 0), banks_b[0])
-        cast_v(("x", 1, 0), 0, 1)
-        cast_v(("x", 1, 0), 1, 2)
-        cast_s(("x", 1, 0), 2, 4)
+        split(("x", 1, 0), 96)
         quant(("x", 1, 0), 0, 1)
         quant(("x", 1, 0), 1, 2)
         quant(("x", 1, 0), 2, 4)
         for i in range(PACK):
             px_pass(0, 1, i)
-        cast_s(("wx", 0, 1), 2, 4)
-        g_stage = sb.tile([P, 2, P, PACK], BF16, name="g_stage", align_bytes=64)
-        for s in range(2):
-            cast_g(g_stage[:, s], raw[("wx", 0, 1)].rearrange("p j (m s) -> p m j s", s=PACK)[:, :, :, s])
+        cast_s(("wx", 0, 1), 1, 4)
+        reuse = stage_of[("x", 1, 0)][:, 3]
+        cast_g(reuse, raw[("wx", 0, 1)].rearrange("p j (m s) -> p m j s", s=PACK)[:, :, :, 0])
         h_mult(0, 0, banks_a[0])
         h_mult(0, 1, banks_a[1])
         warm(2, ("wx", 0, 0), ("x", 0, 0), banks_a[1])
         h_mult(0, 2, banks_a[2])
         warm(2, ("wx", 0, 0), ("x", 0, 0), banks_a[2])
         h_mult(0, 3, banks_a[3])
-        quant(("wx", 0, 1), 2, 4)
         nc.vector.quantize_mx(
-            out=codes[("wx", 0, 1)][:, :2 * P].bitcast(E4M3),
-            scales=scales[("wx", 0, 1)][:, :2 * P],
-            in_=g_stage[:].rearrange("p s m j -> p (s m j)"),
+            out=codes[("wx", 0, 1)][:, :P].bitcast(E4M3),
+            scales=scales[("wx", 0, 1)][:, :P],
+            in_=reuse.rearrange("p m j -> p (m j)"),
         )
+        quant(("wx", 0, 1), 1, 2)
         for i in range(PACK):
-            px_pass(1, 0, i)
-        split(("wx", 1, 1), 96)
+            px_pass(1, 0, i, 0, 2)
+        split(("wx", 1, 1), 112)
+        quant(("wx", 0, 1), 2, 4)
         quant(("wx", 1, 1), 0, 2)
         quant(("wx", 1, 1), 2, 4)
-
         for i in range(PACK):
+            px_pass(1, 0, i, 2, 4)
             px_pass(1, 1, i)
         h_quant(0, 0, 4)
         h_mult(1, 0, banks_a[0])

@@ -143,9 +143,9 @@ def tile_mix_bilin_tm_pl_res_kernel(tc, x, wx, c, wc, w_words, w_scales, prev, o
 
         def h_mult(a, i, bank):
             nc.vector.tensor_tensor(
-                out=h_bf[a][:, i].rearrange("p (u e j) -> p u j e", e=4, j=PACK),
-                in0=bank[:].rearrange("p (j u e) -> p u j e", j=PACK, e=4),
-                in1=pc_sb[a][:, :, i * P:(i + 1) * P].rearrange("p j (u e) -> p u j e", e=4),
+                out=h_bf[a][:, i].rearrange("p (u e j) -> p u j e", e=2, j=PACK),
+                in0=bank[:].rearrange("p (j u e) -> p u j e", j=PACK, e=2),
+                in1=pc_sb[a][:, :, i * P:(i + 1) * P].rearrange("p j (u e) -> p u j e", e=2),
                 op=ALU.mult,
             )
 
@@ -295,15 +295,17 @@ def tile_mix_bilin_tm_pl_res_kernel(tc, x, wx, c, wc, w_words, w_scales, prev, o
         y_pass(1, 3)
         y_add(1, 0, 512)
         nc.sync.dma_start(out=out_rows[:, 1], in_=res[:, 1])
-        y_add(2, 0, 256)
-        y_add(3, 0, 256)
-        o_cast(nc.scalar.copy, 0, 176)
-        y_add(2, 256, 512)
+        y_add(2, 0, 320)
+        y_add(3, 0, 96)
+        o_cast(nc.scalar.copy, 0, 96)
+        y_add(3, 96, 320)
+        o_cast(nc.scalar.copy, 96, 192)
+        y_add(2, 320, 512)
         nc.sync.dma_start(out=out_rows[:, 2], in_=res[:, 2])
-        y_add(3, 256, 512)
+        y_add(3, 320, 512)
         nc.sync.dma_start(out=out_rows[:, 3], in_=res[:, 3])
-        o_cast(nc.vector.tensor_copy, 176, 256)
-        o_cast(nc.vector.tensor_copy, 256, 512)
+        o_cast(nc.vector.tensor_copy, 192, 320)
+        o_cast(nc.vector.tensor_copy, 320, 512)
         o_quant(0, 256)
         store_words(0, 256)
         o_quant(256, 512)

@@ -19,6 +19,14 @@ P = 128
 PACK = 4
 PASS = P * PACK
 WIDE = 512
+STAGES = 4
+
+SCALAR_SHARE = 96
+SCALAR_SHARE_LAST = 112
+
+ADD_CUT = 320
+CAST_START = 96
+CAST_CUT = 192
 
 
 def tile_mix_bilin_tm_pl_res_kernel(tc, x, wx, c, wc, w_words, w_scales, prev, out_0, out_1, out_2):
@@ -29,15 +37,12 @@ def tile_mix_bilin_tm_pl_res_kernel(tc, x, wx, c, wc, w_words, w_scales, prev, o
         ctx.enter_context(tc.manual_schedule())
 
         banks = [ps.tile([P, WIDE], F32, name="bank%d" % b) for b in range(8)]
-        banks_a, banks_b = banks[:4], banks[4:]
+        px_banks, y_banks = banks[:PACK], banks[PACK:]
 
-        def rows(src, g, c0, c1):
-            return src[g * PASS:(g + 1) * PASS, c0:c1].rearrange("(p j) w -> p j w", j=PACK)
-
-        keys = []
-        for g in range(3):
-            keys += [("wc", g, 0), ("wc", g, 1), ("c", g, 0)]
-        keys += [("x", 0, 0), ("wx", 0, 0), ("wx", 1, 0), ("x", 1, 0), ("wx", 0, 1), ("wx", 1, 1)]
+        pieces = []
+        for g in range(L // PASS):
+            pieces += [("wc", g, 0), ("wc", g, 1), ("c", g, 0)]
+        pieces += [("x", 0, 0), ("wx", 0, 0), ("wx", 1, 0), ("x", 1, 0), ("wx", 0, 1), ("wx", 1, 1)]
 
         w_code = sb.tile([P, 2, 2 * M], U8, name="w_code", align_bytes=64)
         w_scale = sb.tile([P, 2, M], U8, name="w_scale", align_bytes=64)
@@ -45,106 +50,96 @@ def tile_mix_bilin_tm_pl_res_kernel(tc, x, wx, c, wc, w_words, w_scales, prev, o
 
         raw, codes, scales = {}, {}, {}
         res = sb.tile([P, PACK, M], F32, name="res", align_bytes=64)
-        for n, key in enumerate(keys):
-            codes[key] = sb.tile([P, WIDE], U32, name="codes%d" % n, align_bytes=64)
-            scales[key] = sb.tile([P, WIDE], U8, name="scales%d" % n, align_bytes=64)
+        for n, piece in enumerate(pieces):
+            codes[piece] = sb.tile([P, WIDE], U32, name="codes%d" % n, align_bytes=64)
+            scales[piece] = sb.tile([P, WIDE], U8, name="scales%d" % n, align_bytes=64)
 
         def load(name, src, g, c0, c1):
             tile = sb.tile([P, PACK, c1 - c0], F32, name="raw_%s%d_%d" % (name, g, c0), align_bytes=64)
-            nc.sync.dma_start(out=tile[:], in_=rows(src, g, c0, c1))
+            rows = src[g * PASS:(g + 1) * PASS, c0:c1]
+            nc.sync.dma_start(out=tile[:], in_=rows.rearrange("(p j) w -> p j w", j=PACK))
             return tile
 
-
-        for g in range(3):
+        for g in range(L // PASS):
             both = load("wc", wc, g, 0, R)
             raw[("wc", g, 0)] = both[:, :, :WIDE]
             raw[("wc", g, 1)] = both[:, :, WIDE:]
             raw[("c", g, 0)] = load("c", c, g, 0, T)[:]
-        raw[("x", 0, 0)] = load("x", x, 0, 0, T)[:]
-        raw[("wx", 0, 0)] = load("wx", wx, 0, 0, WIDE)[:]
-        raw[("wx", 1, 0)] = load("wx", wx, 1, 0, WIDE)[:]
-        raw[("x", 1, 0)] = load("x", x, 1, 0, T)[:]
-        raw[("wx", 0, 1)] = load("wx", wx, 0, WIDE, R)[:]
-        raw[("wx", 1, 1)] = load("wx", wx, 1, WIDE, R)[:]
+        for name, g, a in pieces[3 * (L // PASS):]:
+            raw[(name, g, a)] = load(name, x if name == "x" else wx, g, a * WIDE, (a + 1) * WIDE)[:]
+
         nc.sync.dma_start(out=w_code[:].bitcast(I32), in_=w_words.rearrange("a p n -> p a n").bitcast(I32))
-        for q in range(4):
+        for quad in range(4):
             nc.sync.dma_start(
-                out=w_scale[32 * q:32 * q + 4].bitcast(I32),
-                in_=w_scales[:, 4 * q:4 * q + 4, :].rearrange("a r n -> r a n").bitcast(I32),
+                out=w_scale[32 * quad:32 * quad + 4].bitcast(I32),
+                in_=w_scales[:, 4 * quad:4 * quad + 4, :].rearrange("a q n -> q a n").bitcast(I32),
             )
         nc.sync.dma_start(out=res[:], in_=prev.rearrange("(p i) n -> p i n", i=PACK))
 
-        staged = [sb.tile([P, PACK, P, PACK], BF16, name="staged%d" % n, align_bytes=64) for n in range(4)]
-        stage_of = {key: staged[n % 4] for n, key in enumerate(keys)}
+        staged = [sb.tile([P, PACK, P, PACK], BF16, name="staged%d" % n, align_bytes=64) for n in range(STAGES)]
+        stage = {piece: staged[n % STAGES] for n, piece in enumerate(pieces)}
 
-        def cast_part(copy, src, dst, s0, s1):
+        def cast(copy, piece, s0, s1, m0=0, m1=P):
             copy(
-                out=dst[:, s0:s1].rearrange("p s m j -> p m j s"),
-                in_=src.rearrange("p j (m s) -> p m j s", s=PACK)[:, :, :, s0:s1],
+                out=stage[piece][:, s0:s1, m0:m1].rearrange("p s m j -> p m j s"),
+                in_=raw[piece][:, :, m0 * PACK:m1 * PACK].rearrange("p j (m s) -> p m j s", s=PACK)[:, :, :, s0:s1],
             )
 
-        def cast_v(key, s0=0, s1=2):
-            cast_part(nc.vector.tensor_copy, raw[key], stage_of[key][:], s0, s1)
+        def cast_shared(piece, share=SCALAR_SHARE):
+            cast(nc.vector.tensor_copy, piece, 0, 2)
+            cast(nc.scalar.copy, piece, 2, PACK, 0, share)
+            cast(nc.vector.tensor_copy, piece, 2, PACK, share, P)
 
-        def cast_s(key, s0=2, s1=4):
-            cast_part(nc.scalar.copy, raw[key], stage_of[key][:], s0, s1)
-
-        def quant_half(key, u, s):
-            cols = slice(s * P + 64 * u, s * P + 64 * (u + 1))
+        def quant_from(piece, s0, s1, values):
             nc.vector.quantize_mx(
-                out=codes[key][:, cols].bitcast(E4M3),
-                scales=scales[key][:, cols],
-                in_=stage_of[key][:, s, 64 * u:64 * (u + 1)].rearrange("p m j -> p (m j)"),
+                out=codes[piece][:, s0 * P:s1 * P].bitcast(E5M2 if piece[0] == "c" else E4M3),
+                scales=scales[piece][:, s0 * P:s1 * P],
+                in_=values,
             )
 
-        def quant(key, s0=0, s1=4):
-            fmt = E5M2 if key[0] == "c" else E4M3
-            nc.vector.quantize_mx(
-                out=codes[key][:, s0 * P:s1 * P].bitcast(fmt),
-                scales=scales[key][:, s0 * P:s1 * P],
-                in_=stage_of[key][:, s0:s1].rearrange("p s m j -> p (s m j)"),
-            )
+        def quant(piece, s0=0, s1=PACK):
+            quant_from(piece, s0, s1, stage[piece][:, s0:s1].rearrange("p s m j -> p (s m j)"))
+
+        def slot(planes, piece, s):
+            return planes[piece][:, s * P:(s + 1) * P]
 
         def pc_pass(a, g):
             for j in range(PACK):
-                cols = slice(j * P, (j + 1) * P)
                 nc.tensor.matmul_mx(
-                    out=banks[4 * a + j][:],
-                    lhsT=codes[("wc", g, a)][:, cols].bitcast(E4M3),
-                    lhsT_scale=scales[("wc", g, a)][:, cols],
+                    out=banks[PACK * a + j][:],
+                    lhsT=slot(codes, ("wc", g, a), j).bitcast(E4M3),
+                    lhsT_scale=slot(scales, ("wc", g, a), j),
                     rhs=codes[("c", g, 0)][:].bitcast(E5M2),
                     rhs_scale=scales[("c", g, 0)][:],
                     start=(g == 0),
-                    stop=(g == 2),
+                    stop=(g == L // PASS - 1),
                 )
 
         pc_sb = [sb.tile([P, PACK, T], F32, name="pc_sb%d" % a, align_bytes=64) for a in range(2)]
 
         def pc_copy(a, j):
-            nc.scalar.copy(out=pc_sb[a][:, j], in_=banks[4 * a + j][:])
+            nc.scalar.copy(out=pc_sb[a][:, j], in_=banks[PACK * a + j][:])
 
         def px_pass(a, g, i, j0=0, j1=PACK):
-            tcols = slice(i * P, (i + 1) * P)
             for j in range(j0, j1):
-                cols = slice(j * P, (j + 1) * P)
                 nc.tensor.matmul_mx(
-                    out=banks_a[i][:, cols],
-                    lhsT=codes[("wx", g, a)][:, cols].bitcast(E4M3),
-                    lhsT_scale=scales[("wx", g, a)][:, cols],
-                    rhs=codes[("x", g, 0)][:, tcols].bitcast(E4M3),
-                    rhs_scale=scales[("x", g, 0)][:, tcols],
+                    out=px_banks[i][:, j * P:(j + 1) * P],
+                    lhsT=slot(codes, ("wx", g, a), j).bitcast(E4M3),
+                    lhsT_scale=slot(scales, ("wx", g, a), j),
+                    rhs=slot(codes, ("x", g, 0), i).bitcast(E4M3),
+                    rhs_scale=slot(scales, ("x", g, 0), i),
                     start=(g == 0 and j == 0),
-                    stop=(g == 1 and j == PACK - 1),
+                    stop=(g == K // PASS - 1 and j == PACK - 1),
                 )
 
         h_bf = [sb.tile([P, PACK, P * PACK], BF16, name="h_bf%d" % a, align_bytes=64) for a in range(2)]
         h_code = [sb.tile([P, T], U32, name="h_code%d" % a, align_bytes=64) for a in range(2)]
         h_scale = [sb.tile([P, T], U8, name="h_scale%d" % a, align_bytes=64) for a in range(2)]
 
-        def h_mult(a, i, bank):
+        def h_mult(a, i):
             nc.vector.tensor_tensor(
                 out=h_bf[a][:, i].rearrange("p (u e j) -> p u j e", e=2, j=PACK),
-                in0=bank[:].rearrange("p (j u e) -> p u j e", j=PACK, e=2),
+                in0=px_banks[i][:].rearrange("p (j u e) -> p u j e", j=PACK, e=2),
                 in1=pc_sb[a][:, :, i * P:(i + 1) * P].rearrange("p j (u e) -> p u j e", e=2),
                 op=ALU.mult,
             )
@@ -156,34 +151,27 @@ def tile_mix_bilin_tm_pl_res_kernel(tc, x, wx, c, wc, w_words, w_scales, prev, o
                 in_=h_bf[a][:, i0:i1].rearrange("p i w -> p (i w)"),
             )
 
-        def y_pass(a, i):
-            cols = slice(i * P, (i + 1) * P)
-            nc.tensor.matmul_mx(
-                out=banks_b[i][:],
-                lhsT=h_code[a][:, cols].bitcast(E4M3),
-                lhsT_scale=h_scale[a][:, cols],
-                rhs=w_code[:, a].bitcast(E2M1),
-                rhs_scale=w_scale[:, a],
-                start=(a == 0),
-                stop=(a == 1),
-            )
+        def y_passes(i):
+            for a in range(2):
+                nc.tensor.matmul_mx(
+                    out=y_banks[i][:],
+                    lhsT=h_code[a][:, i * P:(i + 1) * P].bitcast(E4M3),
+                    lhsT_scale=h_scale[a][:, i * P:(i + 1) * P],
+                    rhs=w_code[:, a].bitcast(E2M1),
+                    rhs_scale=w_scale[:, a],
+                    start=(a == 0),
+                    stop=(a == 1),
+                )
 
-        out_rows = out_0.rearrange("(p i) n -> p i n", i=PACK)
+        def y_add(i, n0=0, n1=M):
+            nc.vector.tensor_tensor(out=res[:, i, n0:n1], in0=y_banks[i][:, n0:n1], in1=res[:, i, n0:n1], op=ALU.add)
 
-        def y_add(i, n0, n1):
-            nc.vector.tensor_tensor(out=res[:, i, n0:n1], in0=banks_b[i][:, n0:n1], in1=res[:, i, n0:n1], op=ALU.add)
-
-        def store_res(n0, n1):
-            nc.sync.dma_start(out=out_rows[:, :, n0:n1], in_=res[:, :, n0:n1])
-
-        def shared(key):
-            cast_v(key)
-            cast_s(key)
+        def store_rows(i0, i1):
+            nc.sync.dma_start(out=out_0.rearrange("(p i) n -> p i n", i=PACK)[:, i0:i1], in_=res[:, i0:i1])
 
         o_bf = sb.tile([P, M * PACK], BF16, name="o_bf", align_bytes=64)
         o_code = sb.tile([P, M], U32, name="o_code", align_bytes=64)
         o_scale = sb.tile([P, M], U8, name="o_scale", align_bytes=64)
-        words = out_1[0].rearrange("p n i -> p (n i)").bitcast(I32)
 
         def o_cast(copy, n0, n1):
             copy(
@@ -191,125 +179,112 @@ def tile_mix_bilin_tm_pl_res_kernel(tc, x, wx, c, wc, w_words, w_scales, prev, o
                 in_=res[:, :, n0:n1].rearrange("p i (u e) -> p u i e", e=4),
             )
 
-        def o_quant(n0, n1):
+        def o_quant_and_store(n0, n1):
             nc.vector.quantize_mx(out=o_code[:, n0:n1].bitcast(E4M3), scales=o_scale[:, n0:n1], in_=o_bf[:, n0 * PACK:n1 * PACK])
-
-        def store_words(n0, n1):
+            words = out_1[0].rearrange("p n i -> p (n i)").bitcast(I32)
             nc.sync.dma_start(out=words[:, n0:n1], in_=o_code[:, n0:n1].bitcast(I32))
 
-
-        def split(key, cut):
-            cast_v(key)
-            cast_part(nc.scalar.copy, raw[key][:, :, :cut * PACK], stage_of[key][:, :, :cut], 2, 4)
-            if cut < P:
-                cast_part(nc.vector.tensor_copy, raw[key][:, :, cut * PACK:], stage_of[key][:, :, cut:], 2, 4)
-
-        def cast_g(out, in_):
-            nc.gpsimd.tensor_scalar(out=out, in0=in_, scalar1=1.0, scalar2=0.0, op0=ALU.mult, op1=ALU.add)
-
-
-        def warm(count, wkey, xkey, bank):
+        def warm(count, weights, bank):
             for n in range(count):
                 nc.tensor.matmul_mx(
                     out=bank[:],
-                    lhsT=codes[wkey][:, :P].bitcast(E4M3),
-                    lhsT_scale=scales[wkey][:, :P],
-                    rhs=codes[xkey][:].bitcast(E4M3),
-                    rhs_scale=scales[xkey][:],
+                    lhsT=slot(codes, weights, 0).bitcast(E4M3),
+                    lhsT_scale=slot(scales, weights, 0),
+                    rhs=codes[("x", 0, 0)][:].bitcast(E4M3),
+                    rhs_scale=scales[("x", 0, 0)][:],
                     start=True,
                     stop=True,
                 )
 
-        for g in range(3):
-            split(("wc", g, 0), 96)
-            split(("wc", g, 1), 96)
+        for g in range(L // PASS):
+            cast_shared(("wc", g, 0))
+            cast_shared(("wc", g, 1))
             quant(("wc", g, 0))
             quant(("wc", g, 1))
-            split(("c", g, 0), 96)
+            cast_shared(("c", g, 0))
             quant(("c", g, 0))
             pc_pass(0, g)
             pc_pass(1, g)
-        split(("x", 0, 0), 96)
+
+        cast_shared(("x", 0, 0))
         for j in range(PACK):
             pc_copy(0, j)
         quant(("x", 0, 0))
-        cast_v(("wx", 0, 0), 0, 4)
+        cast(nc.vector.tensor_copy, ("wx", 0, 0), 0, PACK)
         pc_copy(1, 0)
         pc_copy(1, 1)
         quant(("wx", 0, 0))
         for i in range(PACK):
             px_pass(0, 0, i)
-        split(("wx", 1, 0), 96)
+
+        cast_shared(("wx", 1, 0))
         pc_copy(1, 2)
         pc_copy(1, 3)
         quant(("wx", 1, 0))
-        warm(3, ("wx", 1, 0), ("x", 0, 0), banks_b[0])
-        split(("x", 1, 0), 96)
+        warm(3, ("wx", 1, 0), y_banks[0])
+        cast_shared(("x", 1, 0))
         quant(("x", 1, 0), 0, 1)
         quant(("x", 1, 0), 1, 2)
-        quant(("x", 1, 0), 2, 4)
+        quant(("x", 1, 0), 2, PACK)
         for i in range(PACK):
             px_pass(0, 1, i)
-        cast_s(("wx", 0, 1), 1, 4)
-        reuse = stage_of[("x", 1, 0)][:, 3]
-        cast_g(reuse, raw[("wx", 0, 1)].rearrange("p j (m s) -> p m j s", s=PACK)[:, :, :, 0])
-        h_mult(0, 0, banks_a[0])
-        h_mult(0, 1, banks_a[1])
-        warm(2, ("wx", 0, 0), ("x", 0, 0), banks_a[1])
-        h_mult(0, 2, banks_a[2])
-        warm(2, ("wx", 0, 0), ("x", 0, 0), banks_a[2])
-        h_mult(0, 3, banks_a[3])
-        nc.vector.quantize_mx(
-            out=codes[("wx", 0, 1)][:, :P].bitcast(E4M3),
-            scales=scales[("wx", 0, 1)][:, :P],
-            in_=reuse.rearrange("p m j -> p (m j)"),
+
+        cast(nc.scalar.copy, ("wx", 0, 1), 1, PACK)
+        freed = stage[("x", 1, 0)][:, PACK - 1]
+        nc.gpsimd.tensor_scalar(
+            out=freed,
+            in0=raw[("wx", 0, 1)].rearrange("p j (m s) -> p m j s", s=PACK)[:, :, :, 0],
+            scalar1=1.0,
+            scalar2=0.0,
+            op0=ALU.mult,
+            op1=ALU.add,
         )
+        for i in range(PACK):
+            h_mult(0, i)
+            if i in (1, 2):
+                warm(2, ("wx", 0, 0), px_banks[i])
+        quant_from(("wx", 0, 1), 0, 1, freed.rearrange("p m j -> p (m j)"))
         quant(("wx", 0, 1), 1, 2)
         for i in range(PACK):
             px_pass(1, 0, i, 0, 2)
-        split(("wx", 1, 1), 112)
-        quant(("wx", 0, 1), 2, 4)
+
+        cast_shared(("wx", 1, 1), SCALAR_SHARE_LAST)
+        quant(("wx", 0, 1), 2, PACK)
         quant(("wx", 1, 1), 0, 2)
-        quant(("wx", 1, 1), 2, 4)
+        quant(("wx", 1, 1), 2, 3)
+        quant(("wx", 1, 1), 3, PACK)
         for i in range(PACK):
-            px_pass(1, 0, i, 2, 4)
+            px_pass(1, 0, i, 2, PACK)
             px_pass(1, 1, i)
-        h_quant(0, 0, 4)
-        h_mult(1, 0, banks_a[0])
-        h_mult(1, 1, banks_a[1])
-        h_quant(1, 0, 1)
-        y_pass(0, 0)
-        y_pass(1, 0)
-        h_mult(1, 2, banks_a[2])
-        h_quant(1, 1, 2)
-        y_pass(0, 1)
-        y_pass(1, 1)
-        h_mult(1, 3, banks_a[3])
-        h_quant(1, 2, 3)
-        y_pass(0, 2)
-        y_pass(1, 2)
-        y_add(0, 0, 512)
-        nc.sync.dma_start(out=out_rows[:, 0], in_=res[:, 0])
-        h_quant(1, 3, 4)
-        y_pass(0, 3)
-        y_pass(1, 3)
-        y_add(1, 0, 512)
-        nc.sync.dma_start(out=out_rows[:, 1], in_=res[:, 1])
-        y_add(2, 0, 320)
-        y_add(3, 0, 96)
-        o_cast(nc.scalar.copy, 0, 96)
-        y_add(3, 96, 320)
-        o_cast(nc.scalar.copy, 96, 192)
-        y_add(2, 320, 512)
-        nc.sync.dma_start(out=out_rows[:, 2], in_=res[:, 2])
-        y_add(3, 320, 512)
-        nc.sync.dma_start(out=out_rows[:, 3], in_=res[:, 3])
-        o_cast(nc.vector.tensor_copy, 192, 320)
-        o_cast(nc.vector.tensor_copy, 320, 512)
-        o_quant(0, 256)
-        store_words(0, 256)
-        o_quant(256, 512)
-        store_words(256, 512)
-        for q in range(4):
-            eng = nc.sync if q % 2 == 0 else nc.scalar
-            eng.dma_start(out=out_2[0, 4 * q:4 * q + 4, :].bitcast(I32), in_=o_scale[32 * q:32 * q + 4, :].bitcast(I32))
+        h_quant(0, 0, PACK)
+
+        h_mult(1, 0)
+        for i in range(PACK):
+            if i + 1 < PACK:
+                h_mult(1, i + 1)
+            else:
+                y_add(0)
+            h_quant(1, i, i + 1)
+            y_passes(i)
+        y_add(1)
+        store_rows(0, 2)
+
+        y_add(2, 0, ADD_CUT)
+        y_add(3, 0, CAST_START)
+        o_cast(nc.scalar.copy, 0, CAST_START)
+        y_add(3, CAST_START, ADD_CUT)
+        o_cast(nc.scalar.copy, CAST_START, CAST_CUT)
+        for i in (2, 3):
+            y_add(i, ADD_CUT, M)
+        store_rows(2, PACK)
+        o_cast(nc.vector.tensor_copy, CAST_CUT, ADD_CUT)
+        o_cast(nc.vector.tensor_copy, ADD_CUT, M)
+
+        o_quant_and_store(0, M // 2)
+        o_quant_and_store(M // 2, M)
+        for quad in range(4):
+            queue = nc.sync if quad % 2 == 0 else nc.scalar
+            queue.dma_start(
+                out=out_2[0, 4 * quad:4 * quad + 4, :].bitcast(I32),
+                in_=o_scale[32 * quad:32 * quad + 4, :].bitcast(I32),
+            )

@@ -24,9 +24,12 @@ STAGES = 4
 SCALAR_SHARE = 96
 SCALAR_SHARE_LAST = 112
 
+ORDER = (0, 1, 2, 3)
+POOL_CUT = 352
+
+CAST_START = 112
+CAST_CUT = 208
 ADD_CUT = 320
-CAST_START = 96
-CAST_CUT = 192
 
 
 def tile_mix_bilin_tm_pl_res_kernel(tc, x, wx, c, wc, w_words, w_scales, prev, out_0, out_1, out_2):
@@ -151,17 +154,16 @@ def tile_mix_bilin_tm_pl_res_kernel(tc, x, wx, c, wc, w_words, w_scales, prev, o
                 in_=h_bf[a][:, i0:i1].rearrange("p i w -> p (i w)"),
             )
 
-        def y_passes(i):
-            for a in range(2):
-                nc.tensor.matmul_mx(
-                    out=y_banks[i][:],
-                    lhsT=h_code[a][:, i * P:(i + 1) * P].bitcast(E4M3),
-                    lhsT_scale=h_scale[a][:, i * P:(i + 1) * P],
-                    rhs=w_code[:, a].bitcast(E2M1),
-                    rhs_scale=w_scale[:, a],
-                    start=(a == 0),
-                    stop=(a == 1),
-                )
+        def y_pass(i, a):
+            nc.tensor.matmul_mx(
+                out=y_banks[i][:],
+                lhsT=h_code[a][:, i * P:(i + 1) * P].bitcast(E4M3),
+                lhsT_scale=h_scale[a][:, i * P:(i + 1) * P],
+                rhs=w_code[:, a].bitcast(E2M1),
+                rhs_scale=w_scale[:, a],
+                start=(a == 0),
+                stop=(a == 1),
+            )
 
         def y_add(i, n0=0, n1=M):
             nc.vector.tensor_tensor(out=res[:, i, n0:n1], in0=y_banks[i][:, n0:n1], in1=res[:, i, n0:n1], op=ALU.add)
@@ -253,30 +255,45 @@ def tile_mix_bilin_tm_pl_res_kernel(tc, x, wx, c, wc, w_words, w_scales, prev, o
         quant(("wx", 1, 1), 0, 2)
         quant(("wx", 1, 1), 2, 3)
         quant(("wx", 1, 1), 3, PACK)
-        for i in range(PACK):
+        for i in ORDER:
             px_pass(1, 0, i, 2, PACK)
             px_pass(1, 1, i)
         h_quant(0, 0, PACK)
 
-        h_mult(1, 0)
-        for i in range(PACK):
-            if i + 1 < PACK:
-                h_mult(1, i + 1)
-            else:
-                y_add(0)
-            h_quant(1, i, i + 1)
-            y_passes(i)
-        y_add(1)
-        store_rows(0, 2)
+        first, second, third, last = ORDER
+        h_mult(1, first)
+        h_mult(1, second)
+        h_quant(1, first, first + 1)
+        y_pass(first, 0)
+        y_pass(first, 1)
+        y_sb = sb.tile([P, POOL_CUT], F32, name="y_sb", align_bytes=64)
+        nc.scalar.copy(out=y_sb[:], in_=y_banks[first][:, :POOL_CUT])
+        h_mult(1, third)
+        h_quant(1, second, second + 1)
+        y_pass(second, 0)
+        y_pass(second, 1)
+        h_mult(1, last)
+        h_quant(1, third, third + 1)
+        h_quant(1, last, last + 1)
+        y_pass(third, 0)
+        y_pass(last, 0)
+        y_pass(third, 1)
+        y_pass(last, 1)
 
-        y_add(2, 0, ADD_CUT)
-        y_add(3, 0, CAST_START)
+        for n0, n1 in ((0, CAST_CUT), (CAST_CUT, POOL_CUT)):
+            nc.gpsimd.tensor_tensor(out=res[:, first, n0:n1], in0=y_sb[:, n0:n1], in1=res[:, first, n0:n1], op=ALU.add)
+        y_add(second)
+        store_rows(second, second + 1)
+        y_add(first, POOL_CUT, M)
+        store_rows(first, first + 1)
+        y_add(third, 0, CAST_CUT)
+        y_add(last, 0, CAST_START)
         o_cast(nc.scalar.copy, 0, CAST_START)
-        y_add(3, CAST_START, ADD_CUT)
+        y_add(last, CAST_START, ADD_CUT)
         o_cast(nc.scalar.copy, CAST_START, CAST_CUT)
-        for i in (2, 3):
-            y_add(i, ADD_CUT, M)
-        store_rows(2, PACK)
+        y_add(third, CAST_CUT, M)
+        y_add(last, ADD_CUT, M)
+        store_rows(third, last + 1)
         o_cast(nc.vector.tensor_copy, CAST_CUT, ADD_CUT)
         o_cast(nc.vector.tensor_copy, ADD_CUT, M)
 

@@ -25,10 +25,10 @@ SCALAR_SHARE = 96
 SCALAR_SHARE_LAST = 112
 
 ORDER = (0, 1, 2, 3)
-POOL_CUT = 352
+POOL_CUT = 224
 
-CAST_START = 112
-CAST_CUT = 208
+CAST_START = 128
+CAST_CUT = 224
 ADD_CUT = 320
 
 
@@ -135,13 +135,17 @@ def tile_mix_bilin_tm_pl_res_kernel(tc, x, wx, c, wc, w_words, w_scales, prev, o
                     stop=(g == K // PASS - 1 and j == PACK - 1),
                 )
 
-        h_bf = [sb.tile([P, PACK, P * PACK], BF16, name="h_bf%d" % a, align_bytes=64) for a in range(2)]
+        h_first = sb.tile([P, PACK, P * PACK], BF16, name="h_first", align_bytes=64)
+        h_bf = [
+            [h_first[:, i] for i in range(PACK)],
+            [sb.tile([P, P * PACK], BF16, name="h_second%d" % i, align_bytes=64) for i in range(PACK)],
+        ]
         h_code = [sb.tile([P, T], U32, name="h_code%d" % a, align_bytes=64) for a in range(2)]
         h_scale = [sb.tile([P, T], U8, name="h_scale%d" % a, align_bytes=64) for a in range(2)]
 
         def h_mult(a, i):
             nc.vector.tensor_tensor(
-                out=h_bf[a][:, i].rearrange("p (u e j) -> p u j e", e=2, j=PACK),
+                out=h_bf[a][i][:].rearrange("p (u e j) -> p u j e", e=2, j=PACK),
                 in0=px_banks[i][:].rearrange("p (j u e) -> p u j e", j=PACK, e=2),
                 in1=pc_sb[a][:, :, i * P:(i + 1) * P].rearrange("p j (u e) -> p u j e", e=2),
                 op=ALU.mult,
@@ -151,7 +155,7 @@ def tile_mix_bilin_tm_pl_res_kernel(tc, x, wx, c, wc, w_words, w_scales, prev, o
             nc.vector.quantize_mx(
                 out=h_code[a][:, i0 * P:i1 * P].bitcast(E4M3),
                 scales=h_scale[a][:, i0 * P:i1 * P],
-                in_=h_bf[a][:, i0:i1].rearrange("p i w -> p (i w)"),
+                in_=h_first[:, i0:i1].rearrange("p i w -> p (i w)") if a == 0 else h_bf[a][i0][:],
             )
 
         def y_pass(i, a):
@@ -266,8 +270,6 @@ def tile_mix_bilin_tm_pl_res_kernel(tc, x, wx, c, wc, w_words, w_scales, prev, o
         h_quant(1, first, first + 1)
         y_pass(first, 0)
         y_pass(first, 1)
-        y_sb = sb.tile([P, POOL_CUT], F32, name="y_sb", align_bytes=64)
-        nc.scalar.copy(out=y_sb[:], in_=y_banks[first][:, :POOL_CUT])
         h_mult(1, third)
         h_quant(1, second, second + 1)
         y_pass(second, 0)
@@ -275,25 +277,27 @@ def tile_mix_bilin_tm_pl_res_kernel(tc, x, wx, c, wc, w_words, w_scales, prev, o
         h_mult(1, last)
         h_quant(1, third, third + 1)
         h_quant(1, last, last + 1)
+        y_sb = h_bf[1][third][:].bitcast(F32)
+        nc.scalar.copy(out=y_sb[:, :POOL_CUT], in_=y_banks[second][:, :POOL_CUT])
         y_pass(third, 0)
         y_pass(last, 0)
         y_pass(third, 1)
         y_pass(last, 1)
 
-        for n0, n1 in ((0, CAST_CUT), (CAST_CUT, POOL_CUT)):
-            nc.gpsimd.tensor_tensor(out=res[:, first, n0:n1], in0=y_sb[:, n0:n1], in1=res[:, first, n0:n1], op=ALU.add)
-        y_add(second)
-        store_rows(second, second + 1)
-        y_add(first, POOL_CUT, M)
+        nc.gpsimd.tensor_tensor(out=res[:, second, :POOL_CUT], in0=y_sb[:, :POOL_CUT], in1=res[:, second, :POOL_CUT], op=ALU.add)
+        y_add(first)
         store_rows(first, first + 1)
-        y_add(third, 0, CAST_CUT)
+        y_add(second, POOL_CUT, M)
+        store_rows(second, second + 1)
+        y_add(third, 0, CAST_START)
         y_add(last, 0, CAST_START)
         o_cast(nc.scalar.copy, 0, CAST_START)
+        y_add(third, CAST_START, M)
+        store_rows(third, third + 1)
         y_add(last, CAST_START, ADD_CUT)
         o_cast(nc.scalar.copy, CAST_START, CAST_CUT)
-        y_add(third, CAST_CUT, M)
         y_add(last, ADD_CUT, M)
-        store_rows(third, last + 1)
+        store_rows(last, last + 1)
         o_cast(nc.vector.tensor_copy, CAST_CUT, ADD_CUT)
         o_cast(nc.vector.tensor_copy, ADD_CUT, M)
 

@@ -23,6 +23,7 @@ STAGES = 4
 
 SCALAR_SHARE = 96
 SCALAR_SHARE_LAST = 112
+SCALAR_SHARE_COPIES = 64
 
 ORDER = (0, 1, 2, 3)
 POOL_CUT = 224
@@ -213,21 +214,22 @@ def tile_mix_bilin_tm_pl_res_kernel(tc, x, wx, c, wc, w_words, w_scales, prev, o
             pc_pass(1, g)
 
         cast_shared(("x", 0, 0))
-        for j in range(PACK):
+        for j in range(2):
             pc_copy(0, j)
+        for j in range(PACK):
+            pc_copy(1, j)
         quant(("x", 0, 0))
         cast(nc.vector.tensor_copy, ("wx", 0, 0), 0, PACK)
-        pc_copy(1, 0)
-        pc_copy(1, 1)
         quant(("wx", 0, 0))
-        for i in range(PACK):
+        for i in range(2):
             px_pass(0, 0, i)
 
-        cast_shared(("wx", 1, 0))
-        pc_copy(1, 2)
-        pc_copy(1, 3)
+        cast_shared(("wx", 1, 0), SCALAR_SHARE_COPIES)
+        for j in range(2, PACK):
+            pc_copy(0, j)
         quant(("wx", 1, 0))
-        warm(3, ("wx", 1, 0), y_banks[0])
+        for i in range(2, PACK):
+            px_pass(0, 0, i)
         cast_shared(("x", 1, 0))
         quant(("x", 1, 0), 0, 1)
         quant(("x", 1, 0), 1, 2)

@@ -191,18 +191,6 @@ def tile_mix_bilin_tm_pl_res_kernel(tc, x, wx, c, wc, w_words, w_scales, prev, o
             words = out_1[0].rearrange("p n i -> p (n i)").bitcast(I32)
             nc.sync.dma_start(out=words[:, n0:n1], in_=o_code[:, n0:n1].bitcast(I32))
 
-        def warm(count, weights, bank):
-            for n in range(count):
-                nc.tensor.matmul_mx(
-                    out=bank[:],
-                    lhsT=slot(codes, weights, 0).bitcast(E4M3),
-                    lhsT_scale=slot(scales, weights, 0),
-                    rhs=codes[("x", 0, 0)][:].bitcast(E4M3),
-                    rhs_scale=scales[("x", 0, 0)][:],
-                    start=True,
-                    stop=True,
-                )
-
         for g in range(L // PASS):
             cast_shared(("wc", g, 0))
             cast_shared(("wc", g, 1))
@@ -249,8 +237,6 @@ def tile_mix_bilin_tm_pl_res_kernel(tc, x, wx, c, wc, w_words, w_scales, prev, o
         )
         for i in range(PACK):
             h_mult(0, i)
-            if i in (1, 2):
-                warm(2, ("wx", 0, 0), px_banks[i])
         quant_from(("wx", 0, 1), 0, 1, freed.rearrange("p m j -> p (m j)"))
         quant(("wx", 0, 1), 1, 2)
         for i in range(PACK):

@@ -48,18 +48,18 @@ def tile_mix_bilin_tm_pl_res_kernel(tc, x, wx, c, wc, w_words, w_scales, prev, o
             pieces += [("wc", g, 0), ("wc", g, 1), ("c", g, 0)]
         pieces += [("x", 0, 0), ("wx", 0, 0), ("wx", 1, 0), ("x", 1, 0), ("wx", 0, 1), ("wx", 1, 1)]
 
-        w_code = sb.tile([P, 2, 2 * M], U8, name="w_code", align_bytes=64)
-        w_scale = sb.tile([P, 2, M], U8, name="w_scale", align_bytes=64)
+        w_code = sb.tile([P, 2, 2 * M], U8, name="w_code", align_bytes=256)
+        w_scale = sb.tile([P, 2, M], U8, name="w_scale", align_bytes=256)
         nc.gpsimd.memset(w_scale[:].rearrange("p a n -> p (a n)").bitcast(I32), 0)
 
         raw, codes, scales = {}, {}, {}
-        res = sb.tile([P, PACK, M], F32, name="res", align_bytes=64)
+        res = sb.tile([P, PACK, M], F32, name="res", align_bytes=256)
         for n, piece in enumerate(pieces):
-            codes[piece] = sb.tile([P, WIDE], U32, name="codes%d" % n, align_bytes=64)
-            scales[piece] = sb.tile([P, WIDE], U8, name="scales%d" % n, align_bytes=64)
+            codes[piece] = sb.tile([P, WIDE], U32, name="codes%d" % n, align_bytes=256)
+            scales[piece] = sb.tile([P, WIDE], U8, name="scales%d" % n, align_bytes=256)
 
         def load(name, src, g, c0, c1):
-            tile = sb.tile([P, PACK, c1 - c0], F32, name="raw_%s%d_%d" % (name, g, c0), align_bytes=64)
+            tile = sb.tile([P, PACK, c1 - c0], F32, name="raw_%s%d_%d" % (name, g, c0), align_bytes=256)
             rows = src[g * PASS:(g + 1) * PASS, c0:c1]
             nc.sync.dma_start(out=tile[:], in_=rows.rearrange("(p j) w -> p j w", j=PACK))
             return tile
@@ -80,7 +80,7 @@ def tile_mix_bilin_tm_pl_res_kernel(tc, x, wx, c, wc, w_words, w_scales, prev, o
             )
         nc.sync.dma_start(out=res[:], in_=prev.rearrange("(p i) n -> p i n", i=PACK))
 
-        staged = [sb.tile([P, PACK, P, PACK], BF16, name="staged%d" % n, align_bytes=64) for n in range(STAGES)]
+        staged = [sb.tile([P, PACK, P, PACK], BF16, name="staged%d" % n, align_bytes=256) for n in range(STAGES)]
         stage = {piece: staged[n % STAGES] for n, piece in enumerate(pieces)}
 
         def cast(copy, piece, s0, s1, m0=0, m1=P):
@@ -119,7 +119,7 @@ def tile_mix_bilin_tm_pl_res_kernel(tc, x, wx, c, wc, w_words, w_scales, prev, o
                     stop=(g == L // PASS - 1),
                 )
 
-        pc_sb = [sb.tile([P, PACK, T], F32, name="pc_sb%d" % a, align_bytes=64) for a in range(2)]
+        pc_sb = [sb.tile([P, PACK, T], F32, name="pc_sb%d" % a, align_bytes=256) for a in range(2)]
 
         def pc_copy(a, j):
             nc.scalar.copy(out=pc_sb[a][:, j], in_=banks[PACK * a + j][:])
@@ -136,13 +136,13 @@ def tile_mix_bilin_tm_pl_res_kernel(tc, x, wx, c, wc, w_words, w_scales, prev, o
                     stop=(g == K // PASS - 1 and j == PACK - 1),
                 )
 
-        h_first = sb.tile([P, PACK, P * PACK], BF16, name="h_first", align_bytes=64)
+        h_first = sb.tile([P, PACK, P * PACK], BF16, name="h_first", align_bytes=256)
         h_bf = [
             [h_first[:, i] for i in range(PACK)],
-            [sb.tile([P, P * PACK], BF16, name="h_second%d" % i, align_bytes=64) for i in range(PACK)],
+            [sb.tile([P, P * PACK], BF16, name="h_second%d" % i, align_bytes=256) for i in range(PACK)],
         ]
-        h_code = [sb.tile([P, T], U32, name="h_code%d" % a, align_bytes=64) for a in range(2)]
-        h_scale = [sb.tile([P, T], U8, name="h_scale%d" % a, align_bytes=64) for a in range(2)]
+        h_code = [sb.tile([P, T], U32, name="h_code%d" % a, align_bytes=256) for a in range(2)]
+        h_scale = [sb.tile([P, T], U8, name="h_scale%d" % a, align_bytes=256) for a in range(2)]
 
         def h_mult(a, i):
             nc.vector.tensor_tensor(
@@ -176,9 +176,9 @@ def tile_mix_bilin_tm_pl_res_kernel(tc, x, wx, c, wc, w_words, w_scales, prev, o
         def store_rows(i0, i1):
             nc.sync.dma_start(out=out_0.rearrange("(p i) n -> p i n", i=PACK)[:, i0:i1], in_=res[:, i0:i1])
 
-        o_bf = sb.tile([P, M * PACK], BF16, name="o_bf", align_bytes=64)
-        o_code = sb.tile([P, M], U32, name="o_code", align_bytes=64)
-        o_scale = sb.tile([P, M], U8, name="o_scale", align_bytes=64)
+        o_bf = sb.tile([P, M * PACK], BF16, name="o_bf", align_bytes=256)
+        o_code = sb.tile([P, M], U32, name="o_code", align_bytes=256)
+        o_scale = sb.tile([P, M], U8, name="o_scale", align_bytes=256)
 
         def o_cast(copy, n0, n1):
             copy(

@@ -22,7 +22,7 @@ WIDE = 512
 STAGES = 4
 
 SCALAR_SHARE = 96
-SCALAR_SHARE_LAST = 112
+SCALAR_SHARE_LAST = 48
 SCALAR_SHARE_COPIES = 64
 
 ORDER = (0, 1, 2, 3)
@@ -69,8 +69,10 @@ def tile_mix_bilin_tm_pl_res_kernel(tc, x, wx, c, wc, w_words, w_scales, prev, o
             raw[("wc", g, 0)] = both[:, :, :WIDE]
             raw[("wc", g, 1)] = both[:, :, WIDE:]
             raw[("c", g, 0)] = load("c", c, g, 0, T)[:]
-        for name, g, a in pieces[3 * (L // PASS):]:
+        for name, g, a in pieces[3 * (L // PASS):-2]:
             raw[(name, g, a)] = load(name, x if name == "x" else wx, g, a * WIDE, (a + 1) * WIDE)[:]
+        for piece in pieces[-2:]:
+            raw[piece] = [load("wx", wx, piece[1], WIDE + c0, WIDE + c0 + WIDE // 2)[:] for c0 in (0, WIDE // 2)]
 
         nc.sync.dma_start(out=w_code[:].bitcast(I32), in_=w_words.rearrange("a p n -> p a n").bitcast(I32))
         for quad in range(4):
@@ -82,12 +84,24 @@ def tile_mix_bilin_tm_pl_res_kernel(tc, x, wx, c, wc, w_words, w_scales, prev, o
 
         staged = [sb.tile([P, PACK, P, PACK], BF16, name="staged%d" % n, align_bytes=256) for n in range(STAGES)]
         stage = {piece: staged[n % STAGES] for n, piece in enumerate(pieces)}
+        stage[("wx", 0, 1)] = stage[("x", 1, 0)]
 
         def cast(copy, piece, s0, s1, m0=0, m1=P):
             copy(
                 out=stage[piece][:, s0:s1, m0:m1].rearrange("p s m j -> p m j s"),
                 in_=raw[piece][:, :, m0 * PACK:m1 * PACK].rearrange("p j (m s) -> p m j s", s=PACK)[:, :, :, s0:s1],
             )
+
+        def half_views(piece, half, s0, s1, m0, m1):
+            base = half * (P // 2)
+            return (
+                stage[piece][:, s0:s1, base + m0:base + m1].rearrange("p s m j -> p m j s"),
+                raw[piece][half][:, :, m0 * PACK:m1 * PACK].rearrange("p j (m s) -> p m j s", s=PACK)[:, :, :, s0:s1],
+            )
+
+        def cast_half(copy, piece, half, s0, s1, m0=0, m1=P // 2):
+            out, in_ = half_views(piece, half, s0, s1, m0, m1)
+            copy(out=out, in_=in_)
 
         def cast_shared(piece, share=SCALAR_SHARE):
             cast(nc.vector.tensor_copy, piece, 0, 2)
@@ -225,32 +239,38 @@ def tile_mix_bilin_tm_pl_res_kernel(tc, x, wx, c, wc, w_words, w_scales, prev, o
         for i in range(PACK):
             px_pass(0, 1, i)
 
-        cast(nc.scalar.copy, ("wx", 0, 1), 1, PACK)
-        freed = stage[("x", 1, 0)][:, PACK - 1]
-        nc.gpsimd.tensor_scalar(
-            out=freed,
-            in0=raw[("wx", 0, 1)].rearrange("p j (m s) -> p m j s", s=PACK)[:, :, :, 0],
-            scalar1=1.0,
-            scalar2=0.0,
-            op0=ALU.mult,
-            op1=ALU.add,
-        )
+        second, last = pieces[-2:]
+        cast_half(nc.scalar.copy, second, 0, 0, 2)
+        cast_half(nc.scalar.copy, second, 0, 2, PACK)
+        cast_half(nc.scalar.copy, second, 1, 2, PACK)
+        for s in range(2):
+            out, in_ = half_views(second, 1, s, s + 1, 0, P // 2)
+            nc.gpsimd.tensor_scalar(
+                out=out[:, :, :, 0], in0=in_[:, :, :, 0], scalar1=1.0, scalar2=0.0, op0=ALU.mult, op1=ALU.add
+            )
+        cast_half(nc.scalar.copy, last, 0, 0, 2)
+        cast_half(nc.scalar.copy, last, 0, 2, PACK)
         for i in range(PACK):
             h_mult(0, i)
-        quant_from(("wx", 0, 1), 0, 1, freed.rearrange("p m j -> p (m j)"))
-        quant(("wx", 0, 1), 1, 2)
-        for i in range(PACK):
-            px_pass(1, 0, i, 0, 2)
+        quant(second, 0, 2)
+        quant(second, 2, PACK)
+        for i in range(2):
+            px_pass(1, 0, i)
 
-        cast_shared(("wx", 1, 1), SCALAR_SHARE_LAST)
-        quant(("wx", 0, 1), 2, PACK)
-        quant(("wx", 1, 1), 0, 2)
-        quant(("wx", 1, 1), 2, 3)
-        quant(("wx", 1, 1), 3, PACK)
-        for i in ORDER:
-            px_pass(1, 0, i, 2, PACK)
-            px_pass(1, 1, i)
-        h_quant(0, 0, PACK)
+        cast_half(nc.vector.tensor_copy, last, 1, 0, 2)
+        cast_half(nc.scalar.copy, last, 1, 2, PACK, 0, SCALAR_SHARE_LAST)
+        cast_half(nc.vector.tensor_copy, last, 1, 2, PACK, SCALAR_SHARE_LAST, P // 2)
+        h_quant(0, 0, 2)
+        quant(last, 0, 2)
+        quant(last, 2, 3)
+        quant(last, 3, PACK)
+        px_pass(1, 1, 0)
+        px_pass(1, 0, 2)
+        px_pass(1, 1, 1)
+        px_pass(1, 0, 3)
+        px_pass(1, 1, 2)
+        px_pass(1, 1, 3)
+        h_quant(0, 2, PACK)
 
         first, second, third, last = ORDER
         h_mult(1, first)

@@ -22,7 +22,6 @@ WIDE = 512
 STAGES = 4
 
 SCALAR_SHARE = 96
-SCALAR_SHARE_LAST = 48
 SCALAR_SHARE_COPIES = 64
 
 ORDER = (0, 1, 2, 3)
@@ -117,6 +116,14 @@ def tile_mix_bilin_tm_pl_res_kernel(tc, x, wx, c, wc, w_words, w_scales, prev, o
 
         def quant(piece, s0=0, s1=PACK):
             quant_from(piece, s0, s1, stage[piece][:, s0:s1].rearrange("p s m j -> p (s m j)"))
+
+        def quant_half(piece, half, s):
+            m0, m1 = half * (P // 2), (half + 1) * (P // 2)
+            nc.vector.quantize_mx(
+                out=codes[piece][:, s * P + m0:s * P + m1].bitcast(E4M3),
+                scales=scales[piece][:, s * P + m0:s * P + m1],
+                in_=stage[piece][:, s, m0:m1].rearrange("p m j -> p (m j)"),
+            )
 
         def slot(planes, piece, s):
             return planes[piece][:, s * P:(s + 1) * P]
@@ -232,7 +239,8 @@ def tile_mix_bilin_tm_pl_res_kernel(tc, x, wx, c, wc, w_words, w_scales, prev, o
         quant(("wx", 1, 0))
         for i in range(2, PACK):
             px_pass(0, 0, i)
-        cast_shared(("x", 1, 0))
+        cast(nc.vector.tensor_copy, ("x", 1, 0), 0, 2)
+        cast(nc.scalar.copy, ("x", 1, 0), 2, PACK)
         quant(("x", 1, 0), 0, 1)
         quant(("x", 1, 0), 1, 2)
         quant(("x", 1, 0), 2, PACK)
@@ -258,19 +266,17 @@ def tile_mix_bilin_tm_pl_res_kernel(tc, x, wx, c, wc, w_words, w_scales, prev, o
             px_pass(1, 0, i)
 
         cast_half(nc.vector.tensor_copy, last, 1, 0, 2)
-        cast_half(nc.scalar.copy, last, 1, 2, PACK, 0, SCALAR_SHARE_LAST)
-        cast_half(nc.vector.tensor_copy, last, 1, 2, PACK, SCALAR_SHARE_LAST, P // 2)
-        h_quant(0, 0, 2)
-        quant(last, 0, 2)
-        quant(last, 2, 3)
-        quant(last, 3, PACK)
+        cast_half(nc.scalar.copy, last, 1, 2, PACK)
+        for half in range(2):
+            for s in range(PACK):
+                quant_half(last, half, s)
         px_pass(1, 1, 0)
         px_pass(1, 0, 2)
         px_pass(1, 1, 1)
         px_pass(1, 0, 3)
         px_pass(1, 1, 2)
         px_pass(1, 1, 3)
-        h_quant(0, 2, PACK)
+        h_quant(0, 0, PACK)
 
         first, second, third, last = ORDER
         h_mult(1, first)

from contextlib import ExitStack

import concourse.mybir as mybir

K, L, R, M, T = 1024, 1536, 1024, 512, 512
FLOPS = 2 * T * (K * R + L * R + R * M)

F32 = mybir.dt.float32
BF16 = mybir.dt.bfloat16
U32 = mybir.dt.uint32
I32 = mybir.dt.int32
U8 = mybir.dt.uint8
E4M3 = mybir.dt.float8_e4m3fn_x4
E5M2 = mybir.dt.float8_e5m2_x4
E2M1 = mybir.dt.float4_e2m1fn_x4
ALU = mybir.AluOpType

P = 128
PACK = 4
PASS = P * PACK
WIDE = 512
STAGES = 4

SCALAR_SHARE = 96
SCALAR_SHARE_COPIES = 64

ORDER = (0, 1, 2, 3)
POOL_CUT = 224

CAST_START = 128
CAST_CUT = 224
ADD_CUT = 320


def tile_mix_bilin_tm_pl_res_kernel(tc, x, wx, c, wc, w_words, w_scales, prev, out_0, out_1, out_2):
    nc = tc.nc
    with ExitStack() as ctx:
        sb = ctx.enter_context(tc.tile_pool(name="sb", bufs=1))
        ps = ctx.enter_context(tc.psum_pool(name="ps", bufs=1))
        ctx.enter_context(tc.manual_schedule())

        banks = [ps.tile([P, WIDE], F32, name="bank%d" % b) for b in range(8)]
        px_banks, y_banks = banks[:PACK], banks[PACK:]

        pieces = []
        for g in range(L // PASS):
            pieces += [("wc", g, 0), ("wc", g, 1), ("c", g, 0)]
        pieces += [("x", 0, 0), ("wx", 0, 0), ("wx", 1, 0), ("x", 1, 0), ("wx", 0, 1), ("wx", 1, 1)]

        w_code = sb.tile([P, 2, 2 * M], U8, name="w_code", align_bytes=256)
        w_scale = sb.tile([P, 2, M], U8, name="w_scale", align_bytes=256)
        nc.gpsimd.memset(w_scale[:].rearrange("p a n -> p (a n)").bitcast(I32), 0)

        raw, codes, scales = {}, {}, {}
        res = sb.tile([P, PACK, M], F32, name="res", align_bytes=256)
        for n, piece in enumerate(pieces):
            codes[piece] = sb.tile([P, WIDE], U32, name="codes%d" % n, align_bytes=256)
            scales[piece] = sb.tile([P, WIDE], U8, name="scales%d" % n, align_bytes=256)

        def load(name, src, g, c0, c1):
            tile = sb.tile([P, PACK, c1 - c0], F32, name="raw_%s%d_%d" % (name, g, c0), align_bytes=256)
            rows = src[g * PASS:(g + 1) * PASS, c0:c1]
            nc.sync.dma_start(out=tile[:], in_=rows.rearrange("(p j) w -> p j w", j=PACK))
            return tile

        for g in range(L // PASS):
            both = load("wc", wc, g, 0, R)
            raw[("wc", g, 0)] = both[:, :, :WIDE]
            raw[("wc", g, 1)] = both[:, :, WIDE:]
            raw[("c", g, 0)] = load("c", c, g, 0, T)[:]
        for name, g, a in pieces[3 * (L // PASS):-2]:
            raw[(name, g, a)] = load(name, x if name == "x" else wx, g, a * WIDE, (a + 1) * WIDE)[:]
        for piece in pieces[-2:]:
            raw[piece] = [load("wx", wx, piece[1], WIDE + c0, WIDE + c0 + WIDE // 2)[:] for c0 in (0, WIDE // 2)]

        nc.sync.dma_start(out=w_code[:].bitcast(I32), in_=w_words.rearrange("a p n -> p a n").bitcast(I32))
        for quad in range(4):
            nc.sync.dma_start(
                out=w_scale[32 * quad:32 * quad + 4].bitcast(I32),
                in_=w_scales[:, 4 * quad:4 * quad + 4, :].rearrange("a q n -> q a n").bitcast(I32),
            )
        nc.sync.dma_start(out=res[:], in_=prev.rearrange("(p i) n -> p i n", i=PACK))

        staged = [sb.tile([P, PACK, P, PACK], BF16, name="staged%d" % n, align_bytes=256) for n in range(STAGES)]
        stage = {piece: staged[n % STAGES] for n, piece in enumerate(pieces)}
        stage[("wx", 0, 1)] = stage[("x", 1, 0)]

        def cast(copy, piece, s0, s1, m0=0, m1=P):
            copy(
                out=stage[piece][:, s0:s1, m0:m1].rearrange("p s m j -> p m j s"),
                in_=raw[piece][:, :, m0 * PACK:m1 * PACK].rearrange("p j (m s) -> p m j s", s=PACK)[:, :, :, s0:s1],
            )

        def half_views(piece, half, s0, s1, m0, m1):
            base = half * (P // 2)
            return (
                stage[piece][:, s0:s1, base + m0:base + m1].rearrange("p s m j -> p m j s"),
                raw[piece][half][:, :, m0 * PACK:m1 * PACK].rearrange("p j (m s) -> p m j s", s=PACK)[:, :, :, s0:s1],
            )

        def cast_half(copy, piece, half, s0, s1, m0=0, m1=P // 2):
            out, in_ = half_views(piece, half, s0, s1, m0, m1)
            copy(out=out, in_=in_)

        def cast_shared(piece, share=SCALAR_SHARE):
            cast(nc.vector.tensor_copy, piece, 0, 2)
            cast(nc.scalar.copy, piece, 2, PACK, 0, share)
            cast(nc.vector.tensor_copy, piece, 2, PACK, share, P)

        def quant_from(piece, s0, s1, values):
            nc.vector.quantize_mx(
                out=codes[piece][:, s0 * P:s1 * P].bitcast(E5M2 if piece[0] == "c" else E4M3),
                scales=scales[piece][:, s0 * P:s1 * P],
                in_=values,
            )

        def quant(piece, s0=0, s1=PACK):
            quant_from(piece, s0, s1, stage[piece][:, s0:s1].rearrange("p s m j -> p (s m j)"))

        def quant_half(piece, half, s):
            m0, m1 = half * (P // 2), (half + 1) * (P // 2)
            nc.vector.quantize_mx(
                out=codes[piece][:, s * P + m0:s * P + m1].bitcast(E4M3),
                scales=scales[piece][:, s * P + m0:s * P + m1],
                in_=stage[piece][:, s, m0:m1].rearrange("p m j -> p (m j)"),
            )

        def slot(planes, piece, s):
            return planes[piece][:, s * P:(s + 1) * P]

        def pc_pass(a, g):
            for j in range(PACK):
                nc.tensor.matmul_mx(
                    out=banks[PACK * a + j][:],
                    lhsT=slot(codes, ("wc", g, a), j).bitcast(E4M3),
                    lhsT_scale=slot(scales, ("wc", g, a), j),
                    rhs=codes[("c", g, 0)][:].bitcast(E5M2),
                    rhs_scale=scales[("c", g, 0)][:],
                    start=(g == 0),
                    stop=(g == L // PASS - 1),
                )

        pc_sb = [sb.tile([P, PACK, T], F32, name="pc_sb%d" % a, align_bytes=256) for a in range(2)]

        def pc_copy(a, j):
            nc.scalar.copy(out=pc_sb[a][:, j], in_=banks[PACK * a + j][:])

        def px_pass(a, g, i, j0=0, j1=PACK):
            for j in range(j0, j1):
                nc.tensor.matmul_mx(
                    out=px_banks[i][:, j * P:(j + 1) * P],
                    lhsT=slot(codes, ("wx", g, a), j).bitcast(E4M3),
                    lhsT_scale=slot(scales, ("wx", g, a), j),
                    rhs=slot(codes, ("x", g, 0), i).bitcast(E4M3),
                    rhs_scale=slot(scales, ("x", g, 0), i),
                    start=(g == 0 and j == 0),
                    stop=(g == K // PASS - 1 and j == PACK - 1),
                )

        h_first = sb.tile([P, PACK, P * PACK], BF16, name="h_first", align_bytes=256)
        h_bf = [
            [h_first[:, i] for i in range(PACK)],
            [sb.tile([P, P * PACK], BF16, name="h_second%d" % i, align_bytes=256) for i in range(PACK)],
        ]
        h_code = [sb.tile([P, T], U32, name="h_code%d" % a, align_bytes=256) for a in range(2)]
        h_scale = [sb.tile([P, T], U8, name="h_scale%d" % a, align_bytes=256) for a in range(2)]

        def h_mult(a, i):
            nc.vector.tensor_tensor(
                out=h_bf[a][i][:].rearrange("p (u e j) -> p u j e", e=2, j=PACK),
                in0=px_banks[i][:].rearrange("p (j u e) -> p u j e", j=PACK, e=2),
                in1=pc_sb[a][:, :, i * P:(i + 1) * P].rearrange("p j (u e) -> p u j e", e=2),
                op=ALU.mult,
            )

        def h_quant(a, i0, i1):
            nc.vector.quantize_mx(
                out=h_code[a][:, i0 * P:i1 * P].bitcast(E4M3),
                scales=h_scale[a][:, i0 * P:i1 * P],
                in_=h_first[:, i0:i1].rearrange("p i w -> p (i w)") if a == 0 else h_bf[a][i0][:],
            )

        def y_pass(i, a):
            nc.tensor.matmul_mx(
                out=y_banks[i][:],
                lhsT=h_code[a][:, i * P:(i + 1) * P].bitcast(E4M3),
                lhsT_scale=h_scale[a][:, i * P:(i + 1) * P],
                rhs=w_code[:, a].bitcast(E2M1),
                rhs_scale=w_scale[:, a],
                start=(a == 0),
                stop=(a == 1),
            )

        def y_add(i, n0=0, n1=M):
            nc.vector.tensor_tensor(out=res[:, i, n0:n1], in0=y_banks[i][:, n0:n1], in1=res[:, i, n0:n1], op=ALU.add)

        def store_rows(i0, i1):
            nc.sync.dma_start(out=out_0.rearrange("(p i) n -> p i n", i=PACK)[:, i0:i1], in_=res[:, i0:i1])

        o_bf = sb.tile([P, M * PACK], BF16, name="o_bf", align_bytes=256)
        o_code = sb.tile([P, M], U32, name="o_code", align_bytes=256)
        o_scale = sb.tile([P, M], U8, name="o_scale", align_bytes=256)

        def o_cast(copy, n0, n1):
            copy(
                out=o_bf[:, n0 * PACK:n1 * PACK].rearrange("p (u e i) -> p u i e", e=4, i=PACK),
                in_=res[:, :, n0:n1].rearrange("p i (u e) -> p u i e", e=4),
            )

        def o_quant_and_store(n0, n1):
            nc.vector.quantize_mx(out=o_code[:, n0:n1].bitcast(E4M3), scales=o_scale[:, n0:n1], in_=o_bf[:, n0 * PACK:n1 * PACK])
            words = out_1[0].rearrange("p n i -> p (n i)").bitcast(I32)
            nc.sync.dma_start(out=words[:, n0:n1], in_=o_code[:, n0:n1].bitcast(I32))

        for g in range(L // PASS):
            cast_shared(("wc", g, 0))
            cast_shared(("wc", g, 1))
            quant(("wc", g, 0))
            quant(("wc", g, 1))
            cast_shared(("c", g, 0))
            quant(("c", g, 0))
            pc_pass(0, g)
            pc_pass(1, g)

        cast_shared(("x", 0, 0))
        for j in range(2):
            pc_copy(0, j)
        for j in range(PACK):
            pc_copy(1, j)
        quant(("x", 0, 0))
        cast(nc.vector.tensor_copy, ("wx", 0, 0), 0, PACK)
        quant(("wx", 0, 0))
        for i in range(2):
            px_pass(0, 0, i)

        cast_shared(("wx", 1, 0), SCALAR_SHARE_COPIES)
        for j in range(2, PACK):
            pc_copy(0, j)
        quant(("wx", 1, 0))
        for i in range(2, PACK):
            px_pass(0, 0, i)
        cast(nc.vector.tensor_copy, ("x", 1, 0), 0, 2)
        cast(nc.scalar.copy, ("x", 1, 0), 2, PACK)
        quant(("x", 1, 0), 0, 1)
        quant(("x", 1, 0), 1, 2)
        quant(("x", 1, 0), 2, PACK)
        for i in range(PACK):
            px_pass(0, 1, i)

        second, last = pieces[-2:]
        cast_half(nc.scalar.copy, second, 0, 0, 2)
        cast_half(nc.scalar.copy, second, 0, 2, PACK)
        cast_half(nc.scalar.copy, second, 1, 2, PACK)
        for s in range(2):
            out, in_ = half_views(second, 1, s, s + 1, 0, P // 2)
            nc.gpsimd.tensor_scalar(
                out=out[:, :, :, 0], in0=in_[:, :, :, 0], scalar1=1.0, scalar2=0.0, op0=ALU.mult, op1=ALU.add
            )
        cast_half(nc.scalar.copy, last, 0, 0, 2)
        cast_half(nc.scalar.copy, last, 0, 2, PACK)
        for i in range(PACK):
            h_mult(0, i)
        quant(second, 0, 2)
        quant(second, 2, PACK)
        for i in range(2):
            px_pass(1, 0, i)

        cast_half(nc.vector.tensor_copy, last, 1, 0, 2)
        cast_half(nc.scalar.copy, last, 1, 2, PACK)
        for half in range(2):
            for s in range(PACK):
                quant_half(last, half, s)
        px_pass(1, 1, 0)
        px_pass(1, 0, 2)
        px_pass(1, 1, 1)
        px_pass(1, 0, 3)
        px_pass(1, 1, 2)
        px_pass(1, 1, 3)
        h_quant(0, 0, PACK)

        first, second, third, last = ORDER
        h_mult(1, first)
        h_mult(1, second)
        h_quant(1, first, first + 1)
        y_pass(first, 0)
        y_pass(first, 1)
        h_mult(1, third)
        h_quant(1, second, second + 1)
        y_pass(second, 0)
        y_pass(second, 1)
        h_mult(1, last)
        h_quant(1, third, third + 1)
        h_quant(1, last, last + 1)
        y_sb = h_bf[1][third][:].bitcast(F32)
        nc.scalar.copy(out=y_sb[:, :POOL_CUT], in_=y_banks[second][:, :POOL_CUT])
        y_pass(third, 0)
        y_pass(last, 0)
        y_pass(third, 1)
        y_pass(last, 1)

        nc.gpsimd.tensor_tensor(out=res[:, second, :POOL_CUT], in0=y_sb[:, :POOL_CUT], in1=res[:, second, :POOL_CUT], op=ALU.add)
        y_add(first)
        store_rows(first, first + 1)
        y_add(second, POOL_CUT, M)
        store_rows(second, second + 1)
        y_add(third, 0, CAST_START)
        y_add(last, 0, CAST_START)
        o_cast(nc.scalar.copy, 0, CAST_START)
        y_add(third, CAST_START, M)
        store_rows(third, third + 1)
        y_add(last, CAST_START, ADD_CUT)
        o_cast(nc.scalar.copy, CAST_START, CAST_CUT)
        y_add(last, ADD_CUT, M)
        store_rows(last, last + 1)
        o_cast(nc.vector.tensor_copy, CAST_CUT, ADD_CUT)
        o_cast(nc.vector.tensor_copy, ADD_CUT, M)

        o_quant_and_store(0, M // 2)
        o_quant_and_store(M // 2, M)
        for quad in range(4):
            queue = nc.sync if quad % 2 == 0 else nc.scalar
            queue.dma_start(
                out=out_2[0, 4 * quad:4 * quad + 4, :].bitcast(I32),
                in_=o_scale[32 * quad:32 * quad + 4, :].bitcast(I32),
            )
